import numpy as np
import ml_dtypes


def mxq(x, axis, fmt="e4m3"):
    dtype, down = {"e4m3": (ml_dtypes.float8_e4m3fn, 7), "e5m2": (ml_dtypes.float8_e5m2, 14)}[fmt]
    v = np.moveaxis(np.asarray(x, np.float32).astype(ml_dtypes.bfloat16).astype(np.float64), axis, -1)
    blocks = v.reshape(v.shape[:-1] + (-1, 32))
    amax = np.abs(blocks).max(-1, keepdims=True)
    byte = np.maximum(np.where(amax > 0, np.frexp(amax)[1] - 1 + 127, 0) - down, 1)
    scale = np.exp2(byte - 127.0)
    codes = (blocks / scale).astype(np.float32).astype(dtype).astype(np.float64)
    return np.moveaxis((codes * scale).reshape(v.shape), -1, axis)


WIDE = False


def mx_kscale(k):
    if not WIDE:
        return np.ones(k)
    levels = np.array([10, -10, 5, -5, 0])
    if k % 512:
        return np.exp2(np.random.permutation(np.resize(levels, k // 32))).repeat(32)
    a = np.empty((k // 512, 16))
    for p in range(k // 512):
        a[p, :8] = np.random.permutation(np.resize(levels, 8))
        for g in range(8):
            far = levels[np.abs(levels - a[p, g]) >= 10]
            a[p, g + 8] = far[np.random.randint(len(far))]
    return np.exp2(a.ravel()).repeat(32)


BF16 = ml_dtypes.bfloat16


def bf(x):
    return np.asarray(x, np.float32).astype(BF16)


def f64(x):
    return np.asarray(x).astype(np.float64)


E2M1 = np.array([0.0, 0.5, 1.0, 1.5, 2.0, 3.0, 4.0, 6.0, -0.0, -0.5, -1.0, -1.5, -2.0, -3.0, -4.0, -6.0])


def pack_weight(w, fmt):
    k, n = w.shape
    w = f64(bf(w)).reshape(k // 32, 32, n)
    amax = np.abs(w).max(1)
    if fmt == "e4m3":
        byte = np.frexp(amax)[1] - 1 + 127 - 7
    else:
        mant, ex = np.frexp(amax / 6.0)
        byte = np.where(mant > 0.5, ex, ex - 1) + 127
    byte = np.clip(np.where(amax > 0, byte, 1), 1, 254)
    scaled = (w * np.exp2(127.0 - byte)[:, None, :]).reshape(k, n).astype(np.float32)
    by_word = np.ascontiguousarray(scaled.reshape(k // 512, 128, 4, n).transpose(0, 1, 3, 2))
    if fmt == "e4m3":
        words = by_word.astype(ml_dtypes.float8_e4m3fn).view(np.uint8)
    else:
        c = by_word.astype(ml_dtypes.float4_e2m1fn).view(np.uint8) & 0xF
        words = c[..., 0::2] | (c[..., 1::2] << 4)
    return np.ascontiguousarray(words), np.ascontiguousarray(byte.astype(np.uint8).reshape(k // 512, 16, n))


def unpack_weight(words, scales, fmt):
    g, p, n, _ = words.shape
    if fmt == "e4m3":
        vals = np.ascontiguousarray(words).view(ml_dtypes.float8_e4m3fn).astype(np.float64)
    else:
        nib = np.empty((g, p, n, 4), np.uint8)
        nib[..., 0::2] = words & 0xF
        nib[..., 1::2] = words >> 4
        vals = E2M1[nib]
    vals = vals * np.repeat(np.exp2(scales.astype(np.float64) - 127.0), 8, axis=1)[..., None]
    return vals.transpose(0, 1, 3, 2).reshape(g * 512, n)


T, D, F = 2048, 1024, 1024


def erf(u):
    c = np.clip(u, -6.0, 6.0)
    q = 2.0 * c * c
    term = np.array(c)
    total = np.array(c)
    for n in range(1, 151):
        term *= q / (2 * n + 1)
        total += term
    return np.where(np.abs(u) > 6.0, np.sign(u), 2.0 / np.sqrt(np.pi) * np.exp(-c * c) * total)


def gelu_erf_grad(a):
    cdf = 0.5 * (1.0 + erf(a / np.sqrt(2.0)))
    pdf_term = a * np.exp(-np.square(a) / 2.0) / np.sqrt(2.0 * np.pi)
    return cdf + pdf_term


def frobenius(z):
    return np.sqrt(np.sum(np.square(z), axis=(0, 1)))


def draw0():
    s, t = mx_kscale(D), mx_kscale(T)
    x = bf(np.random.standard_normal((T, D)) / t[:, None])
    a = bf(np.random.standard_normal((T, F)))
    dy = bf(np.random.standard_normal((T, D)) * s[None, :] * t[:, None])
    w2_words, w2_scales = pack_weight((np.random.standard_normal((F, D)) / np.sqrt(D) / s[None, :]).T, "e4m3")
    return {
        "x": x,
        "a": a,
        "dy": dy,
        "w2_words": w2_words,
        "w2_scales": w2_scales,
        "w1": bf(np.random.standard_normal((D, F))),
        "m": bf(np.random.standard_normal((D, F)) * 0.3),
        "v": bf(np.random.uniform(0.2, 1.0, (D, F))),
    }


def core(x, a, dy, w2_words, w2_scales, w1, m, v):
    x, a, dy, w1, m, v = f64(x), f64(a), f64(dy), f64(w1), f64(m), f64(v)
    tokens = x.shape[0]
    dh = mxq(dy, 1, "e4m3") @ unpack_weight(w2_words, w2_scales, "e4m3")
    da = dh * gelu_erf_grad(a)
    g = (mxq(x, 0, "e4m3").T @ mxq(da, 0, "e4m3")) / np.sqrt(tokens)
    m_new = 0.6 * m + 0.4 * g
    v_new = 0.6 * v + 0.4 * np.square(g)
    r = m_new / np.sqrt(v_new) + 0.1 * w1
    trust = frobenius(w1) / frobenius(r)
    return w1 - 0.5 * trust * r


def e4m3fn_bytes(y):
    return np.clip(np.asarray(y, np.float64), -448.0, 448.0).astype(np.float32).astype(ml_dtypes.float8_e4m3fn).view(np.uint8)


def e4m3fn_values(b):
    return np.asarray(b, np.uint8).view(ml_dtypes.float8_e4m3fn).astype(np.float64)


def setup_inputs():
    d = draw0()
    x0 = np.asarray(d['x']).astype(np.float64)
    s = (np.max(np.abs(x0), axis=(1,), keepdims=True) / 448.0).astype(np.float32)
    out = {}
    for k, v in d.items():
        if k == 'x':
            out['x_bytes'] = e4m3fn_bytes(x0 / s.astype(np.float64))
            out['x_scale'] = s
        else:
            out[k] = v
    return out


def reference(x_bytes, x_scale, a, dy, w2_words, w2_scales, w1, m, v):
    return core(e4m3fn_values(x_bytes) * x_scale.astype(np.float64), a, dy, w2_words, w2_scales, w1, m, v)

@@ -1,0 +1,412 @@
+import math
+from contextlib import ExitStack
+
+import concourse.mybir as mybir
+from concourse.masks import make_identity
+
+T, D, F = 2048, 1024, 1024
+FLOPS = 2 * T * D * F * 2
+
+F32 = mybir.dt.float32
+BF16 = mybir.dt.bfloat16
+U32 = mybir.dt.uint32
+U8 = mybir.dt.uint8
+I32 = mybir.dt.int32
+FP8 = mybir.dt.float8_e4m3fn
+X4 = mybir.dt.float8_e4m3fn_x4
+ALU = mybir.AluOpType
+ACT = mybir.ActivationFunctionType
+
+P = 128
+NG = 4
+NM = 8
+FH = 512
+FS = 256
+
+LAM = 1.0 + 8.0 / 2**23
+H = 2422.0 / 2**20
+NU = 417.0 / 512
+C = -8.395447793042201e-07
+A = (1.0 - 2.0 * C) / (2.0 * H)
+CR = C / A
+CLAMP = 8.0
+DY_ON_V = {(0, 0), (0, 1)}
+X_ON_V = {(0, 0)}
+
+G2_SCALE = math.sqrt(2.0 / 3.0 / T)
+M_SCALE = 2.0 / 3.0 / math.sqrt(T)
+W_SCALE = 0.1 / math.sqrt(0.6)
+
+
+def tile_lambmlpbackwardstep_w8_kernel(tc, x_bytes, x_scale, a, dy, w2_words, w2_scales, w1, m, v, out):
+    nc = tc.nc
+    with ExitStack() as ctx:
+        keep = ctx.enter_context(tc.tile_pool(name="keep", bufs=1))
+        sb = ctx.enter_context(tc.tile_pool(name="sb", bufs=2))
+        ps_dh = ctx.enter_context(tc.psum_pool(name="ps_dh", bufs=3))
+        ps_tr = ctx.enter_context(tc.psum_pool(name="ps_tr", bufs=2))
+        ps_g = ctx.enter_context(tc.psum_pool(name="ps_g", bufs=2))
+        ps_w = ctx.enter_context(tc.psum_pool(name="ps_w", bufs=1))
+
+        ident = keep.tile([P, P], F32, name="ident")
+        ones = keep.tile([P, P], F32, name="ones")
+        xs = keep.tile([P, NG, 4], F32, name="xs")
+        dyc = keep.tile([P, 2, T], U32, name="dyc", align_bytes=64)
+        dys = keep.tile([P, 2, T], U8, name="dys", align_bytes=64)
+        wc = keep.tile([P, 2, F], U32, name="wc", align_bytes=64)
+        ws = keep.tile([P, 2, F], U8, name="ws", align_bytes=64)
+        xc = keep.tile([P, NG, D], U32, name="xc", align_bytes=64)
+        xsc = keep.tile([P, NG, D], U8, name="xsc", align_bytes=64)
+        dac = keep.tile([P, NG, F], U32, name="dac", align_bytes=64)
+        das = keep.tile([P, NG, F], U8, name="das", align_bytes=64)
+        w1t = keep.tile([P, NM, F], BF16, name="w1t")
+        r = keep.tile([P, NM, F], F32, name="r")
+        stats = keep.tile([P, 2 * NM], F32, name="stats")
+        small = keep.tile([P, 8], F32, name="small")
+        small2 = keep.tile([P, 8], F32, name="small2")
+
+        a_v = a.rearrange("(g p t) f -> g p t f", p=P, t=4)
+        dy_v = dy.rearrange("(g p t) k -> g p t k", p=P, t=4)
+        x_v = x_bytes.rearrange("(g p t) d -> g p t d", p=P, t=4)
+        xs_v = x_scale.rearrange("(g p t) o -> p g (t o)", p=P, t=4)
+        w1_v = w1.rearrange("(m p) f -> p m f", p=P)
+        m_v = m.rearrange("(m p) f -> p m f", p=P)
+        v_v = v.rearrange("(m p) f -> p m f", p=P)
+        out_v = out.rearrange("(m p) f -> p m f", p=P)
+
+        nc.gpsimd.memset(ws[:].rearrange("p c n -> p (c n)").bitcast(I32), 0)
+        make_identity(nc, ident[:])
+        nc.gpsimd.memset(ones[:], 1.0)
+
+        a_tiles, dy_tiles, x_tiles, mv_tiles = {}, {}, {}, {}
+
+        def load_a(h, g):
+            t = sb.tile([P, 4, FH], BF16, name="at", bufs=3)
+            a_tiles[h, g] = t
+            parts = 2 if (h, g) == (0, 0) else 1
+            w = FH // parts
+            for i in range(parts):
+                nc.sync.dma_start(out=t[:, :, i * w : (i + 1) * w], in_=a_v[g][:, :, h * FH + i * w : h * FH + (i + 1) * w])
+
+        def load_dy(g):
+            t = sb.tile([P, 4, D], BF16, name="dyt", bufs=2)
+            dy_tiles[g] = t
+            nc.sync.dma_start(out=t[:], in_=dy_v[g])
+
+        def load_x(g):
+            t = sb.tile([P, 4, D], U8, name="xb", bufs=2)
+            x_tiles[g] = t
+            nc.sync.dma_start(out=t[:], in_=x_v[g])
+
+        def load_w(h):
+            for c in range(2):
+                src = w2_words[c].rearrange("p n t -> p (n t)")[:, 4 * h * FH : 4 * (h + 1) * FH]
+                nc.sync.dma_start(out=wc[:, c, h * FH : (h + 1) * FH].bitcast(I32), in_=src.bitcast(I32))
+
+        def load_mv(h, mm):
+            mt = sb.tile([P, FH], BF16, name="mt", bufs=4)
+            vt = sb.tile([P, FH], BF16, name="vt", bufs=4)
+            mv_tiles[h, mm] = (mt, vt)
+            nc.sync.dma_start(out=mt[:], in_=m_v[:, mm, h * FH : (h + 1) * FH])
+            nc.sync.dma_start(out=vt[:], in_=v_v[:, mm, h * FH : (h + 1) * FH])
+
+        ac_tiles, g_tiles, da_tiles, vn_tiles = {}, {}, {}, {}
+
+        def clamp(i):
+            h, g, q = i // 8, (i // 2) % 4, i % 2
+            ac = sb.tile([P, 4, FS], BF16, name="ac", bufs=3)
+            ac_tiles[i] = ac
+            src = a_tiles[h, g][:, :, q * FS : (q + 1) * FS]
+            nc.vector.tensor_scalar(
+                out=ac[:],
+                in0=src,
+                scalar1=CLAMP,
+                scalar2=-CLAMP,
+                op0=ALU.min,
+                op1=ALU.max,
+            )
+
+        def s_gelu(i):
+            src = ac_tiles[i][:].rearrange("p t f -> p (t f)")
+            gp = sb.tile([P, 4 * FS], F32, name="gp", bufs=3)
+            gm = sb.tile([P, 4 * FS], F32, name="gm", bufs=2)
+            th = sb.tile([P, 4 * FS], BF16, name="th", bufs=2)
+            g_tiles[i] = (gp, gm, th)
+            nc.scalar.activation(out=gp[:], in_=src, func=ACT.Gelu, scale=LAM, bias=H)
+            nc.scalar.activation(out=gm[:], in_=src, func=ACT.Gelu, scale=LAM, bias=-H)
+            nc.scalar.activation(out=th[:], in_=src, func=ACT.Tanh, scale=NU)
+
+        def pe_dh(i):
+            h, g, q = i // 8, (i // 2) % 4, i % 2
+            banks = []
+            for b in range(2):
+                dh = ps_dh.tile([P, 4, P], F32, name="dh")
+                banks.append(dh)
+                f0 = h * FH + q * FS + b * P
+                for t in range(4):
+                    t0 = g * 512 + t * P
+                    for c in range(2):
+                        nc.tensor.matmul_mx(
+                            out=dh[:, t, :],
+                            lhsT=dyc[:, c, t0 : t0 + P].bitcast(X4),
+                            lhsT_scale=dys[:, c, t0 : t0 + P],
+                            rhs=wc[:, c, f0 : f0 + P].bitcast(X4),
+                            rhs_scale=ws[:, c, f0 : f0 + P],
+                            start=(c == 0),
+                            stop=(c == 1),
+                        )
+            return banks
+
+        def v_diff(i):
+            gp, gm, th = g_tiles[i]
+            nc.vector.scalar_tensor_tensor(out=gp[:], in0=gm[:], scalar=CR, in1=gp[:], op0=ALU.subtract, op1=ALU.subtract)
+
+        def v_third(i):
+            gp, gm, th = g_tiles[i]
+            nc.vector.scalar_tensor_tensor(out=gp[:], in0=th[:], scalar=-CR, in1=gp[:], op0=ALU.mult, op1=ALU.add)
+
+        def v_da(i, banks):
+            gp = g_tiles[i][0]
+            da = sb.tile([P, FS, 4], BF16, name="da", bufs=3, align_bytes=64)
+            da_tiles[i] = da
+            q_v = gp[:].rearrange("p (t f) -> p f t", t=4)
+            for b in range(2):
+                fs = slice(b * P, (b + 1) * P)
+                nc.vector.scalar_tensor_tensor(
+                    out=da[:, fs, :],
+                    in0=banks[b][:].rearrange("p t f -> p f t"),
+                    scalar=-A,
+                    in1=q_v[:, fs, :],
+                    op0=ALU.mult,
+                    op1=ALU.mult,
+                )
+
+        def v_quant_da(i):
+            h, g, q = i // 8, (i // 2) % 4, i % 2
+            f0 = h * FH + q * FS
+            nc.vector.quantize_mx(
+                out=dac[:, g, f0 : f0 + FS].bitcast(X4),
+                scales=das[:, g, f0 : f0 + FS],
+                in_=da_tiles[i][:].rearrange("p f t -> p (f t)"),
+            )
+
+        dyg_tiles = {}
+
+        def dy_transpose(g, c):
+            words = dy_tiles[g][:].bitcast(F32)
+            dyg = sb.tile([P, 512, 4], BF16, name="dyg", bufs=2, align_bytes=64)
+            dyg_tiles[g, c] = dyg
+            dst = dyg[:].rearrange("p n e -> p (n e)").bitcast(F32)
+            for b in range(2):
+                tr = ps_tr.tile([P, 2, 2, P], F32, name="tr")
+                for tt in range(2):
+                    for u in range(2):
+                        nc.tensor.transpose(tr[:, tt, u, :], words[:, 2 * b + tt, 256 * c + u : 256 * (c + 1) : 2], ident[:])
+                copy = nc.vector.tensor_copy if (g, c) in DY_ON_V else nc.scalar.copy
+                copy(
+                    out=dst[:, b * 512 : (b + 1) * 512].rearrange("p (t m u) -> p t m u", t=2, u=2),
+                    in_=tr[:].rearrange("p t u m -> p t m u"),
+                )
+
+        def dy_quant(g, c):
+            nc.vector.quantize_mx(
+                out=dyc[:, c, g * 512 : (g + 1) * 512].bitcast(X4),
+                scales=dys[:, c, g * 512 : (g + 1) * 512],
+                in_=dyg_tiles[g, c][:].rearrange("p n e -> p (n e)"),
+            )
+
+        xw_tiles, xi_tiles = {}, {}
+
+        def x_widen(g, e):
+            xw = sb.tile([P, 4, 512], BF16, name="xw", bufs=2)
+            xw_tiles[g, e] = xw
+            for t in range(4):
+                src = x_tiles[g][:, t, e * 512 : (e + 1) * 512].bitcast(FP8)
+                if (g, e) in X_ON_V:
+                    nc.vector.tensor_scalar(out=xw[:, t, :], in0=src, scalar1=xs[:, g, t : t + 1], scalar2=None, op0=ALU.mult)
+                else:
+                    nc.scalar.activation(out=xw[:, t, :], in_=src, func=ACT.Copy, scale=xs[:, g, t : t + 1])
+
+        def x_interleave(g, e):
+            xi = sb.tile([P, 512, 4], BF16, name="xi", bufs=2, align_bytes=64)
+            xi_tiles[g, e] = xi
+            nc.vector.tensor_copy(
+                out=xi[:].rearrange("p (c i) t -> p c t i", i=4),
+                in_=xw_tiles[g, e][:].rearrange("p t (c i) -> p c t i", i=4),
+            )
+
+        def x_quant(g, e):
+            nc.vector.quantize_mx(
+                out=xc[:, g, e * 512 : (e + 1) * 512].bitcast(X4),
+                scales=xsc[:, g, e * 512 : (e + 1) * 512],
+                in_=xi_tiles[g, e][:].rearrange("p n t -> p (n t)"),
+            )
+
+        def epi_front(h, mm):
+            fs = slice(h * FH, (h + 1) * FH)
+            ms = slice(mm * P, (mm + 1) * P)
+            gps = ps_g.tile([P, FH], F32, name="gps")
+            for g in range(NG):
+                nc.tensor.matmul_mx(
+                    out=gps[:],
+                    lhsT=xc[:, g, ms].bitcast(X4),
+                    lhsT_scale=xsc[:, g, ms],
+                    rhs=dac[:, g, fs].bitcast(X4),
+                    rhs_scale=das[:, g, fs],
+                    start=(g == 0),
+                    stop=(g == NG - 1),
+                )
+            mt = mv_tiles[h, mm][0]
+            if h == 0:
+                vn = r[:, mm, FH:]
+            else:
+                vn = sb.tile([P, FH], F32, name="vn", bufs=4)[:]
+            vn_tiles[h, mm] = vn
+            nc.scalar.activation(out=vn, in_=gps[:], func=ACT.Square, scale=G2_SCALE)
+            nc.vector.scalar_tensor_tensor(out=r[:, mm, fs], in0=gps[:], scalar=M_SCALE, in1=mt[:], op0=ALU.mult, op1=ALU.add)
+
+        def epi_vn(h, mm):
+            vn = vn_tiles[h, mm]
+            nc.vector.tensor_tensor(out=vn, in0=mv_tiles[h, mm][1][:], in1=vn, op=ALU.add)
+
+        def epi_rs(h, mm):
+            vn = vn_tiles[h, mm]
+            nc.scalar.activation(out=vn, in_=vn, func=ACT.Abs_reciprocal_sqrt)
+
+        def epi_u(h, mm):
+            fs = slice(h * FH, (h + 1) * FH)
+            nc.vector.tensor_tensor(out=r[:, mm, fs], in0=r[:, mm, fs], in1=vn_tiles[h, mm], op=ALU.mult)
+
+        def epi_r(h, mm):
+            fs = slice(h * FH, (h + 1) * FH)
+            nc.vector.scalar_tensor_tensor(out=r[:, mm, fs], in0=w1t[:, mm, fs], scalar=-W_SCALE, in1=r[:, mm, fs], op0=ALU.mult, op1=ALU.subtract)
+
+        def epi_sq(h, mm):
+            fs = slice(h * FH, (h + 1) * FH)
+            junk = sb.tile([P, FH], BF16, name="junk", bufs=2)
+            j = h * NM + mm
+            nc.scalar.activation(out=junk[:], in_=r[:, mm, fs], func=ACT.Square, accum_out=stats[:, j : j + 1])
+
+        gram = ps_w.tile([P, P], F32, name="gram")
+
+        def w_gram(mm):
+            for b in range(8):
+                blk = w1t[:, mm, b * P : (b + 1) * P]
+                nc.tensor.matmul(out=gram[:], lhsT=blk, rhs=blk, start=(mm == 0 and b == 0), stop=(mm == NM - 1 and b == 7))
+
+        with tc.manual_schedule():
+            load_a(0, 0)
+            load_dy(0)
+            load_w(0)
+            for q in range(4):
+                nc.sync.dma_start(
+                    out=ws[32 * q : 32 * q + 4, :, :].bitcast(I32),
+                    in_=w2_scales[:, 4 * q : 4 * q + 4, :].rearrange("c r n -> r c n").bitcast(I32),
+                )
+            load_a(0, 1)
+            nc.sync.dma_start(out=xs[:], in_=xs_v)
+            load_x(0)
+            load_dy(1)
+            load_x(1)
+            for g in range(2, 4):
+                load_a(0, g)
+                load_dy(g)
+                load_x(g)
+            load_w(1)
+            load_a(1, 0)
+            nc.sync.dma_start(out=w1t[:], in_=w1_v)
+            for g in range(1, 4):
+                load_a(1, g)
+                load_mv(0, g - 1)
+            for mm in range(3, 8):
+                load_mv(0, mm)
+            for mm in range(8):
+                load_mv(1, mm)
+
+            nc.vector.memset(small[:], 0.0)
+            nc.scalar.activation(out=small[:, 0:1], in_=small[:, 1:2], func=ACT.Gelu)
+            clamp(0)
+            clamp(1)
+            s_gelu(0)
+            dy_transpose(0, 0)
+            dy_transpose(0, 1)
+            dy_quant(0, 0)
+            dy_quant(0, 1)
+            x_widen(0, 0)
+
+            for i in range(16):
+                h, g, q = i // 8, (i // 2) % 4, i % 2
+                if i > 0:
+                    s_gelu(i)
+                if h == 0:
+                    if q == 0 and g > 0:
+                        dy_quant(g, 1)
+                    if g < 3:
+                        dy_transpose(g + 1, q)
+                    if i < 7:
+                        x_widen((i + 1) // 2, (i + 1) % 2)
+                banks = pe_dh(i)
+                v_diff(i)
+                if i > 0:
+                    v_quant_da(i - 1)
+                if i + 2 < 16:
+                    clamp(i + 2)
+                v_third(i)
+                if h == 0:
+                    x_interleave(g, q)
+                    if q == 1 and g < 3:
+                        dy_quant(g + 1, 0)
+                v_da(i, banks)
+                if h == 0:
+                    x_quant(g, q)
+                else:
+                    epi_front(0, i - 8)
+                    w_gram(i - 8)
+                    if i > 8:
+                        epi_vn(0, i - 9)
+            for k in range(7):
+                epi_rs(0, k)
+            v_quant_da(15)
+            epi_vn(0, 7)
+            epi_rs(0, 7)
+            scr = sb.tile([P, P], F32, name="scr", bufs=1)
+            nc.vector.tensor_tensor(out=scr[:], in0=gram[:], in1=ident[:], op=ALU.mult)
+
+            epi_u(0, 0)
+            for k in range(9):
+                if k + 1 < 8:
+                    epi_u(0, k + 1)
+                if k < 8:
+                    epi_front(1, k)
+                    epi_r(0, k)
+                    epi_sq(0, k)
+                if k == 0:
+                    nc.vector.tensor_reduce(out=small[:, 2:3], in_=scr[:], op=ALU.add, axis=mybir.AxisListType.X)
+                if k == 2:
+                    tw = ps_tr.tile([P, 1], F32, name="tr")
+                    nc.tensor.matmul(out=tw[:], lhsT=ones[:], rhs=small[:, 2:3], start=True, stop=True)
+                    nc.vector.tensor_scalar(out=small[:, 3:4], in0=tw[:], scalar1=0.25, scalar2=None, op0=ALU.mult)
+                if k == 3:
+                    nc.vector.reciprocal(out=small[:, 4:5], in_=small[:, 3:4])
+                if k > 0:
+                    epi_vn(1, k - 1)
+                    epi_rs(1, k - 1)
+                if k > 2:
+                    epi_u(1, k - 3)
+                if k > 3:
+                    epi_r(1, k - 4)
+                    epi_sq(1, k - 4)
+            for k in range(6, 8):
+                epi_u(1, k)
+                epi_r(1, k - 1)
+                epi_sq(1, k - 1)
+            epi_r(1, 7)
+            epi_sq(1, 7)
+
+            tot = ps_tr.tile([P, 1], F32, name="tr")
+            for j in range(16):
+                nc.tensor.matmul(out=tot[:], lhsT=ones[:], rhs=stats[:, j : j + 1], start=(j == 0), stop=(j == 15))
+            nc.scalar.activation(out=small2[:, 0:1], in_=tot[:], func=ACT.Abs_reciprocal_sqrt, scale=small[:, 4:5])
+            for mm in range(NM):
+                nc.vector.scalar_tensor_tensor(out=r[:, mm, :], in0=r[:, mm, :], scalar=small2[:, 0:1], in1=w1t[:, mm, :], op0=ALU.mult, op1=ALU.add)
+                nc.sync.dma_start(out=out_v[:, mm, :], in_=r[:, mm, :])

@@ -23,18 +23,20 @@ NM = 8
 FH = 512
 FS = 256
 
-LAM = 1.0 + 8.0 / 2**23
-H = 2422.0 / 2**20
-NU = 417.0 / 512
-C = -8.395447793042201e-07
+LAM = 1.0 + 9.0 / 2**23
+H = 2568.0 / 2**20
+NU = 211.0 / 256
+C = -1.0 / 2**20
 A = (1.0 - 2.0 * C) / (2.0 * H)
-CR = C / A
+D_SCALE = -A / C
 CLAMP = 8.0
-DY_ON_V = {(0, 0), (0, 1)}
-X_ON_V = {(0, 0)}
+DY_ON_V = {(g, c, b) for g in range(4) for c in range(2) for b in range(2) if (g, c) != (0, 1)}
+XQ_POS = 1
+DYQ_LATE = 0
+X_PLAN = {(0, 0): "VV-1", (1, 0): "SP1", (2, 0): "SP2", (3, 0): "SP4", (0, 1): "SP6", (1, 1): "SV7", (2, 1): "SV8", (3, 1): "SP9"}
 
-G2_SCALE = math.sqrt(2.0 / 3.0 / T)
-M_SCALE = 2.0 / 3.0 / math.sqrt(T)
+G2_SCALE = C * math.sqrt(2.0 / 3.0 / T)
+M_SCALE = C * 2.0 / 3.0 / math.sqrt(T)
 W_SCALE = 0.1 / math.sqrt(0.6)
 
 
@@ -49,6 +51,7 @@ def tile_lambmlpbackwardstep_w8_kernel(tc, x_bytes, x_scale, a, dy, w2_words, w2
         ps_w = ctx.enter_context(tc.psum_pool(name="ps_w", bufs=1))
 
         ident = keep.tile([P, P], F32, name="ident")
+        identb = keep.tile([P, P], BF16, name="identb")
         ones = keep.tile([P, P], F32, name="ones")
         xs = keep.tile([P, NG, 4], F32, name="xs")
         dyc = keep.tile([P, 2, T], U32, name="dyc", align_bytes=64)
@@ -76,12 +79,13 @@ def tile_lambmlpbackwardstep_w8_kernel(tc, x_bytes, x_scale, a, dy, w2_words, w2
 
         nc.gpsimd.memset(ws[:].rearrange("p c n -> p (c n)").bitcast(I32), 0)
         make_identity(nc, ident[:])
+        make_identity(nc, identb[:])
         nc.gpsimd.memset(ones[:], 1.0)
 
         a_tiles, dy_tiles, x_tiles, mv_tiles = {}, {}, {}, {}
 
         def load_a(h, g):
-            t = sb.tile([P, 4, FH], BF16, name="at", bufs=3)
+            t = sb.tile([P, 4, FH], BF16, name="at", bufs=2)
             a_tiles[h, g] = t
             parts = 2 if (h, g) == (0, 0) else 1
             w = FH // parts
@@ -91,24 +95,28 @@ def tile_lambmlpbackwardstep_w8_kernel(tc, x_bytes, x_scale, a, dy, w2_words, w2
         def load_dy(g):
             t = sb.tile([P, 4, D], BF16, name="dyt", bufs=2)
             dy_tiles[g] = t
-            nc.sync.dma_start(out=t[:], in_=dy_v[g])
+            parts = 2 if g == 0 else 1
+            w = D // parts
+            for i in range(parts):
+                nc.sync.dma_start(out=t[:, :, i * w : (i + 1) * w], in_=dy_v[g][:, :, i * w : (i + 1) * w])
 
-        def load_x(g):
-            t = sb.tile([P, 4, D], U8, name="xb", bufs=2)
-            x_tiles[g] = t
-            nc.sync.dma_start(out=t[:], in_=x_v[g])
+        def load_x(g, e):
+            t = sb.tile([P, 4, 512], U8, name="xb", bufs=3)
+            x_tiles[g, e] = t
+            nc.sync.dma_start(out=t[:], in_=x_v[g][:, :, e * 512 : (e + 1) * 512])
 
         def load_w(h):
             for c in range(2):
                 src = w2_words[c].rearrange("p n t -> p (n t)")[:, 4 * h * FH : 4 * (h + 1) * FH]
                 nc.sync.dma_start(out=wc[:, c, h * FH : (h + 1) * FH].bitcast(I32), in_=src.bitcast(I32))
 
-        def load_mv(h, mm):
-            mt = sb.tile([P, FH], BF16, name="mt", bufs=4)
-            vt = sb.tile([P, FH], BF16, name="vt", bufs=4)
-            mv_tiles[h, mm] = (mt, vt)
-            nc.sync.dma_start(out=mt[:], in_=m_v[:, mm, h * FH : (h + 1) * FH])
-            nc.sync.dma_start(out=vt[:], in_=v_v[:, mm, h * FH : (h + 1) * FH])
+        def load_mv(h, k):
+            mt = sb.tile([P, 2, FH], BF16, name="mt", bufs=2)
+            vt = sb.tile([P, 2, FH], BF16, name="vt", bufs=3)
+            for mm in (2 * k, 2 * k + 1):
+                mv_tiles[h, mm] = (mt, vt)
+            nc.sync.dma_start(out=mt[:], in_=m_v[:, 2 * k : 2 * k + 2, h * FH : (h + 1) * FH])
+            nc.sync.dma_start(out=vt[:], in_=v_v[:, 2 * k : 2 * k + 2, h * FH : (h + 1) * FH])
 
         ac_tiles, g_tiles, da_tiles, vn_tiles = {}, {}, {}, {}
 
@@ -128,7 +136,7 @@ def tile_lambmlpbackwardstep_w8_kernel(tc, x_bytes, x_scale, a, dy, w2_words, w2
 
         def s_gelu(i):
             src = ac_tiles[i][:].rearrange("p t f -> p (t f)")
-            gp = sb.tile([P, 4 * FS], F32, name="gp", bufs=3)
+            gp = sb.tile([P, 4 * FS], F32, name="gp", bufs=2)
             gm = sb.tile([P, 4 * FS], F32, name="gm", bufs=2)
             th = sb.tile([P, 4 * FS], BF16, name="th", bufs=2)
             g_tiles[i] = (gp, gm, th)
@@ -157,27 +165,33 @@ def tile_lambmlpbackwardstep_w8_kernel(tc, x_bytes, x_scale, a, dy, w2_words, w2
                         )
             return banks
 
-        def v_diff(i):
+        d_tiles, q_tiles = {}, {}
+
+        def g_diff(i):
             gp, gm, th = g_tiles[i]
-            nc.vector.scalar_tensor_tensor(out=gp[:], in0=gm[:], scalar=CR, in1=gp[:], op0=ALU.subtract, op1=ALU.subtract)
+            d = sb.tile([P, 4 * FS], F32, name="d", bufs=1)
+            d_tiles[i] = d
+            nc.gpsimd.tensor_tensor(out=d[:], in0=gm[:], in1=gp[:], op=ALU.subtract)
 
         def v_third(i):
-            gp, gm, th = g_tiles[i]
-            nc.vector.scalar_tensor_tensor(out=gp[:], in0=th[:], scalar=-CR, in1=gp[:], op0=ALU.mult, op1=ALU.add)
+            th = g_tiles[i][2]
+            q = sb.tile([P, 4 * FS], F32, name="q", bufs=1)
+            q_tiles[i] = q
+            nc.vector.scalar_tensor_tensor(out=q[:], in0=d_tiles[i][:], scalar=D_SCALE, in1=th[:], op0=ALU.mult, op1=ALU.add)
 
         def v_da(i, banks):
-            gp = g_tiles[i][0]
+            q = q_tiles[i]
             da = sb.tile([P, FS, 4], BF16, name="da", bufs=3, align_bytes=64)
             da_tiles[i] = da
-            q_v = gp[:].rearrange("p (t f) -> p f t", t=4)
+            q_v = q[:].rearrange("p (t f) -> p f t", t=4)
             for b in range(2):
                 fs = slice(b * P, (b + 1) * P)
                 nc.vector.scalar_tensor_tensor(
                     out=da[:, fs, :],
-                    in0=banks[b][:].rearrange("p t f -> p f t"),
-                    scalar=-A,
-                    in1=q_v[:, fs, :],
-                    op0=ALU.mult,
+                    in0=q_v[:, fs, :],
+                    scalar=1.0,
+                    in1=banks[b][:].rearrange("p t f -> p f t"),
+                    op0=ALU.add,
                     op1=ALU.mult,
                 )
 
@@ -192,21 +206,25 @@ def tile_lambmlpbackwardstep_w8_kernel(tc, x_bytes, x_scale, a, dy, w2_words, w2
 
         dyg_tiles = {}
 
+        dy_banks = {}
+
         def dy_transpose(g, c):
             words = dy_tiles[g][:].bitcast(F32)
-            dyg = sb.tile([P, 512, 4], BF16, name="dyg", bufs=2, align_bytes=64)
-            dyg_tiles[g, c] = dyg
-            dst = dyg[:].rearrange("p n e -> p (n e)").bitcast(F32)
+            dyg_tiles[g, c] = sb.tile([P, 512, 4], BF16, name="dyg", bufs=2, align_bytes=64)
             for b in range(2):
                 tr = ps_tr.tile([P, 2, 2, P], F32, name="tr")
+                dy_banks[g, c, b] = tr
                 for tt in range(2):
                     for u in range(2):
                         nc.tensor.transpose(tr[:, tt, u, :], words[:, 2 * b + tt, 256 * c + u : 256 * (c + 1) : 2], ident[:])
-                copy = nc.vector.tensor_copy if (g, c) in DY_ON_V else nc.scalar.copy
-                copy(
-                    out=dst[:, b * 512 : (b + 1) * 512].rearrange("p (t m u) -> p t m u", t=2, u=2),
-                    in_=tr[:].rearrange("p t u m -> p t m u"),
-                )
+
+        def dy_copy(g, c, b):
+            dst = dyg_tiles[g, c][:].rearrange("p n e -> p (n e)").bitcast(F32)
+            copy = nc.vector.tensor_copy if (g, c, b) in DY_ON_V else nc.scalar.copy
+            copy(
+                out=dst[:, b * 512 : (b + 1) * 512].rearrange("p (t m u) -> p t m u", t=2, u=2),
+                in_=dy_banks[g, c, b][:].rearrange("p t u m -> p t m u"),
+            )
 
         def dy_quant(g, c):
             nc.vector.quantize_mx(
@@ -221,19 +239,44 @@ def tile_lambmlpbackwardstep_w8_kernel(tc, x_bytes, x_scale, a, dy, w2_words, w2
             xw = sb.tile([P, 4, 512], BF16, name="xw", bufs=2)
             xw_tiles[g, e] = xw
             for t in range(4):
-                src = x_tiles[g][:, t, e * 512 : (e + 1) * 512].bitcast(FP8)
-                if (g, e) in X_ON_V:
+                src = x_tiles[g, e][:, t, :].bitcast(FP8)
+                if X_PLAN[g, e][0] == "V":
                     nc.vector.tensor_scalar(out=xw[:, t, :], in0=src, scalar1=xs[:, g, t : t + 1], scalar2=None, op0=ALU.mult)
                 else:
                     nc.scalar.activation(out=xw[:, t, :], in_=src, func=ACT.Copy, scale=xs[:, g, t : t + 1])
 
+        x_banks = {}
+
+        def x_transfer(g, e):
+            banks = []
+            for b in range(2):
+                bank = (ps_g if e == 0 else ps_tr).tile([P, 2, P, 4], BF16, name="gps" if e == 0 else "tr")
+                banks.append(bank)
+                for j in range(2):
+                    d0 = (2 * b + j) * P
+                    nc.tensor.matmul(
+                        out=bank[:, j, :, :].rearrange("p d t -> p (d t)"),
+                        lhsT=identb[:],
+                        rhs=xw_tiles[g, e][:, :, d0 : d0 + P].rearrange("p t d -> p d t"),
+                        start=True,
+                        stop=True,
+                    )
+            x_banks[g, e] = banks
+
         def x_interleave(g, e):
             xi = sb.tile([P, 512, 4], BF16, name="xi", bufs=2, align_bytes=64)
             xi_tiles[g, e] = xi
-            nc.vector.tensor_copy(
-                out=xi[:].rearrange("p (c i) t -> p c t i", i=4),
-                in_=xw_tiles[g, e][:].rearrange("p t (c i) -> p c t i", i=4),
-            )
+            if X_PLAN[g, e][1] == "V":
+                nc.vector.tensor_copy(
+                    out=xi[:].rearrange("p (c i) t -> p c t i", i=4),
+                    in_=xw_tiles[g, e][:].rearrange("p t (c i) -> p c t i", i=4),
+                )
+                return
+            for b in range(2):
+                nc.scalar.copy(
+                    out=xi[:, b * 256 : (b + 1) * 256, :].rearrange("p d t -> p (d t)"),
+                    in_=x_banks[g, e][b][:].rearrange("p j d t -> p (j d t)"),
+                )
 
         def x_quant(g, e):
             nc.vector.quantize_mx(
@@ -242,10 +285,13 @@ def tile_lambmlpbackwardstep_w8_kernel(tc, x_bytes, x_scale, a, dy, w2_words, w2
                 in_=xi_tiles[g, e][:].rearrange("p n t -> p (n t)"),
             )
 
-        def epi_front(h, mm):
+        gps_tiles = {}
+        vn_dst = {}
+
+        def epi_front(h, mm, pool=None, name="gps", sq=True):
             fs = slice(h * FH, (h + 1) * FH)
             ms = slice(mm * P, (mm + 1) * P)
-            gps = ps_g.tile([P, FH], F32, name="gps")
+            gps = (pool or ps_g).tile([P, FH], F32, name=name)
             for g in range(NG):
                 nc.tensor.matmul_mx(
                     out=gps[:],
@@ -256,36 +302,58 @@ def tile_lambmlpbackwardstep_w8_kernel(tc, x_bytes, x_scale, a, dy, w2_words, w2
                     start=(g == 0),
                     stop=(g == NG - 1),
                 )
-            mt = mv_tiles[h, mm][0]
             if h == 0:
                 vn = r[:, mm, FH:]
             else:
-                vn = sb.tile([P, FH], F32, name="vn", bufs=4)[:]
-            vn_tiles[h, mm] = vn
-            nc.scalar.activation(out=vn, in_=gps[:], func=ACT.Square, scale=G2_SCALE)
-            nc.vector.scalar_tensor_tensor(out=r[:, mm, fs], in0=gps[:], scalar=M_SCALE, in1=mt[:], op0=ALU.mult, op1=ALU.add)
+                if mm % 2 == 0:
+                    vn_tiles["cur"] = sb.tile([P, 2, FH], F32, name="vn", bufs=3)
+                vn = vn_tiles["cur"][:, mm % 2, :]
+            vn_tiles[h, mm] = vn_tiles.get("cur")
+            gps_tiles[h, mm] = gps
+            vn_dst[h, mm] = vn
+            if sq:
+                epi_g2(h, mm)
 
-        def epi_vn(h, mm):
-            vn = vn_tiles[h, mm]
-            nc.vector.tensor_tensor(out=vn, in0=mv_tiles[h, mm][1][:], in1=vn, op=ALU.add)
+        def epi_g2(h, mm):
+            nc.scalar.activation(out=vn_dst[h, mm], in_=gps_tiles[h, mm][:], func=ACT.Square, scale=G2_SCALE)
 
-        def epi_rs(h, mm):
-            vn = vn_tiles[h, mm]
-            nc.scalar.activation(out=vn, in_=vn, func=ACT.Abs_reciprocal_sqrt)
-
-        def epi_u(h, mm):
+        def epi_mn(h, mm):
+            gps = gps_tiles[h, mm]
             fs = slice(h * FH, (h + 1) * FH)
-            nc.vector.tensor_tensor(out=r[:, mm, fs], in0=r[:, mm, fs], in1=vn_tiles[h, mm], op=ALU.mult)
+            nc.vector.scalar_tensor_tensor(out=r[:, mm, fs], in0=gps[:], scalar=M_SCALE, in1=mv_tiles[h, mm][0][:, mm % 2, :], op0=ALU.mult, op1=ALU.add)
 
-        def epi_r(h, mm):
-            fs = slice(h * FH, (h + 1) * FH)
-            nc.vector.scalar_tensor_tensor(out=r[:, mm, fs], in0=w1t[:, mm, fs], scalar=-W_SCALE, in1=r[:, mm, fs], op0=ALU.mult, op1=ALU.subtract)
+        def vn_of(blk):
+            h, m0, n = blk
+            if h == 0:
+                return r[:, m0 : m0 + n, FH:]
+            return vn_tiles[h, m0][:, m0 % 2 : m0 % 2 + n, :]
 
-        def epi_sq(h, mm):
-            fs = slice(h * FH, (h + 1) * FH)
-            junk = sb.tile([P, FH], BF16, name="junk", bufs=2)
-            j = h * NM + mm
-            nc.scalar.activation(out=junk[:], in_=r[:, mm, fs], func=ACT.Square, accum_out=stats[:, j : j + 1])
+        def r_of(blk):
+            h, m0, n = blk
+            return r[:, m0 : m0 + n, h * FH : (h + 1) * FH]
+
+        def epi_vn(blk):
+            h, m0, n = blk
+            nc.vector.tensor_tensor(out=vn_of(blk), in0=mv_tiles[h, m0][1][:, m0 % 2 : m0 % 2 + n, :], in1=vn_of(blk), op=ALU.add)
+
+        def epi_rs(blk):
+            nc.scalar.activation(out=vn_of(blk), in_=vn_of(blk), func=ACT.Abs_reciprocal_sqrt)
+
+        def epi_u(blk):
+            nc.vector.tensor_tensor(out=r_of(blk), in0=r_of(blk), in1=vn_of(blk), op=ALU.mult)
+
+        def epi_r(blk):
+            h, m0, n = blk
+            nc.vector.scalar_tensor_tensor(out=r_of(blk), in0=w1t[:, m0 : m0 + n, h * FH : (h + 1) * FH], scalar=-W_SCALE, in1=r_of(blk), op0=ALU.mult, op1=ALU.subtract)
+
+        stat_cols = []
+
+        def epi_sq(blk):
+            h, m0, n = blk
+            junk = sb.tile([P, 2, FH], BF16, name="junk", bufs=1)
+            j = len(stat_cols)
+            stat_cols.append(blk)
+            nc.scalar.activation(out=junk[:, 0:n, :], in_=r_of(blk), func=ACT.Square, accum_out=stats[:, j : j + 1])
 
         gram = ps_w.tile([P, P], F32, name="gram")
 
@@ -296,6 +364,8 @@ def tile_lambmlpbackwardstep_w8_kernel(tc, x_bytes, x_scale, a, dy, w2_words, w2
 
         with tc.manual_schedule():
             load_a(0, 0)
+            nc.sync.dma_start(out=xs[:], in_=xs_v)
+            load_x(0, 0)
             load_dy(0)
             load_w(0)
             for q in range(4):
@@ -304,109 +374,167 @@ def tile_lambmlpbackwardstep_w8_kernel(tc, x_bytes, x_scale, a, dy, w2_words, w2
                     in_=w2_scales[:, 4 * q : 4 * q + 4, :].rearrange("c r n -> r c n").bitcast(I32),
                 )
             load_a(0, 1)
-            nc.sync.dma_start(out=xs[:], in_=xs_v)
-            load_x(0)
             load_dy(1)
-            load_x(1)
-            for g in range(2, 4):
-                load_a(0, g)
-                load_dy(g)
-                load_x(g)
+            load_x(1, 0)
+            load_a(0, 2)
+            load_dy(2)
+            load_x(2, 0)
+            load_a(0, 3)
+            load_dy(3)
+            load_x(3, 0)
             load_w(1)
             load_a(1, 0)
+            load_x(0, 1)
+            load_x(1, 1)
+            load_a(1, 1)
             nc.sync.dma_start(out=w1t[:], in_=w1_v)
-            for g in range(1, 4):
-                load_a(1, g)
-                load_mv(0, g - 1)
-            for mm in range(3, 8):
-                load_mv(0, mm)
-            for mm in range(8):
-                load_mv(1, mm)
+            load_mv(0, 0)
+            load_x(2, 1)
+            load_a(1, 2)
+            load_x(3, 1)
+            load_mv(0, 1)
+            load_a(1, 3)
+            load_mv(0, 2)
+            load_mv(0, 3)
+            for k in range(4):
+                load_mv(1, k)
 
             nc.vector.memset(small[:], 0.0)
             nc.scalar.activation(out=small[:, 0:1], in_=small[:, 1:2], func=ACT.Gelu)
             clamp(0)
             clamp(1)
             s_gelu(0)
-            dy_transpose(0, 0)
-            dy_transpose(0, 1)
-            dy_quant(0, 0)
-            dy_quant(0, 1)
             x_widen(0, 0)
+            for c in range(2):
+                dy_transpose(0, c)
+                dy_copy(0, c, 0)
+                dy_copy(0, c, 1)
+            dy_quant(0, 0)
+            x_at = {}
+            for unit, plan in X_PLAN.items():
+                step = int(plan[2:])
+                if unit != (0, 0):
+                    x_at.setdefault((step, "w"), []).append(unit)
+                x_at.setdefault((step + 1, "i" + plan[1]), []).append(unit)
+                x_at.setdefault((step + 2, "q"), []).append(unit)
 
             for i in range(16):
                 h, g, q = i // 8, (i // 2) % 4, i % 2
+                nxt = h == 0 and g < 3
+                for unit in x_at.get((i, "iP"), []):
+                    x_transfer(*unit)
                 if i > 0:
                     s_gelu(i)
-                if h == 0:
-                    if q == 0 and g > 0:
-                        dy_quant(g, 1)
-                    if g < 3:
-                        dy_transpose(g + 1, q)
-                    if i < 7:
-                        x_widen((i + 1) // 2, (i + 1) % 2)
-                banks = pe_dh(i)
-                v_diff(i)
-                if i > 0:
-                    v_quant_da(i - 1)
+                g_diff(i)
+                if nxt:
+                    dy_transpose(g + 1, q)
+                    for b in range(2):
+                        if (g + 1, q, b) not in DY_ON_V:
+                            dy_copy(g + 1, q, b)
+                for unit in x_at.get((i, "iP"), []):
+                    x_interleave(*unit)
+                for unit in x_at.get((i, "w"), []):
+                    x_widen(*unit)
+                if h == 0 and q == 0:
+                    dy_quant(g, 1)
                 if i + 2 < 16:
                     clamp(i + 2)
+                if i > 0:
+                    v_quant_da(i - 1)
+                for unit in x_at.get((i, "iV"), []):
+                    x_interleave(*unit)
+                for unit in x_at.get((i, "q"), []):
+                    x_quant(*unit)
+                if nxt and q == 1:
+                    dy_quant(g + 1, 0)
+                if i in (11, 13, 15):
+                    epi_vn((0, i - 11, 2))
                 v_third(i)
-                if h == 0:
-                    x_interleave(g, q)
-                    if q == 1 and g < 3:
-                        dy_quant(g + 1, 0)
-                v_da(i, banks)
-                if h == 0:
-                    x_quant(g, q)
-                else:
+                if h == 1:
                     epi_front(0, i - 8)
+                banks = pe_dh(i)
+                if nxt and (g + 1, q, 0) in DY_ON_V:
+                    dy_copy(g + 1, q, 0)
+                if h == 1:
+                    epi_mn(0, i - 8)
                     w_gram(i - 8)
-                    if i > 8:
-                        epi_vn(0, i - 9)
-            for k in range(7):
-                epi_rs(0, k)
+                v_da(i, banks)
+                if nxt and (g + 1, q, 1) in DY_ON_V:
+                    dy_copy(g + 1, q, 1)
+            b0 = [(0, 2 * k, 2) for k in range(4)]
+            c0 = [(1, 0, 2), (1, 2, 2), (1, 4, 2), (1, 6, 1), (1, 7, 1)]
+            for k in range(3):
+                epi_rs(b0[k])
             v_quant_da(15)
-            epi_vn(0, 7)
-            epi_rs(0, 7)
+            epi_vn(b0[3])
+            epi_rs(b0[3])
             scr = sb.tile([P, P], F32, name="scr", bufs=1)
             nc.vector.tensor_tensor(out=scr[:], in0=gram[:], in1=ident[:], op=ALU.mult)
+            tail_pool = {0: (ps_g, "gps"), 1: (ps_dh, "dh")}
 
-            epi_u(0, 0)
-            for k in range(9):
-                if k + 1 < 8:
-                    epi_u(0, k + 1)
-                if k < 8:
-                    epi_front(1, k)
-                    epi_r(0, k)
-                    epi_sq(0, k)
-                if k == 0:
-                    nc.vector.tensor_reduce(out=small[:, 2:3], in_=scr[:], op=ALU.add, axis=mybir.AxisListType.X)
-                if k == 2:
-                    tw = ps_tr.tile([P, 1], F32, name="tr")
-                    nc.tensor.matmul(out=tw[:], lhsT=ones[:], rhs=small[:, 2:3], start=True, stop=True)
-                    nc.vector.tensor_scalar(out=small[:, 3:4], in0=tw[:], scalar1=0.25, scalar2=None, op0=ALU.mult)
-                if k == 3:
-                    nc.vector.reciprocal(out=small[:, 4:5], in_=small[:, 3:4])
-                if k > 0:
-                    epi_vn(1, k - 1)
-                    epi_rs(1, k - 1)
-                if k > 2:
-                    epi_u(1, k - 3)
-                if k > 3:
-                    epi_r(1, k - 4)
-                    epi_sq(1, k - 4)
-            for k in range(6, 8):
-                epi_u(1, k)
-                epi_r(1, k - 1)
-                epi_sq(1, k - 1)
-            epi_r(1, 7)
-            epi_sq(1, 7)
+            def front(mm):
+                epi_front(1, mm, *tail_pool[mm % 2])
+                epi_mn(1, mm)
+
+            epi_u(b0[0])
+            epi_u(b0[1])
+            front(0)
+            front(1)
+            epi_r(b0[0])
+            epi_sq(b0[0])
+            epi_vn(c0[0])
+            epi_rs(c0[0])
+            epi_r(b0[1])
+            epi_u(b0[2])
+            front(2)
+            front(3)
+            nc.vector.tensor_reduce(out=small[:, 2:3], in_=scr[:], op=ALU.add, axis=mybir.AxisListType.X)
+            epi_sq(b0[1])
+            epi_r(b0[2])
+            epi_vn(c0[1])
+            epi_rs(c0[1])
+            epi_u(c0[0])
+            epi_u(b0[3])
+            front(4)
+            front(5)
+            epi_sq(b0[2])
+            tw = ps_tr.tile([P, 1], F32, name="tr")
+            nc.tensor.matmul(out=tw[:], lhsT=ones[:], rhs=small[:, 2:3], start=True, stop=True)
+            epi_r(c0[0])
+            epi_vn(c0[2])
+            epi_rs(c0[2])
+            epi_r(b0[3])
+            nc.vector.tensor_scalar(out=small[:, 3:4], in0=tw[:], scalar1=0.25, scalar2=None, op0=ALU.mult)
+            epi_u(c0[1])
+            front(6)
+            front(7)
+            epi_sq(c0[0])
+            epi_r(c0[1])
+            epi_vn(c0[3])
+            epi_rs(c0[3])
+            epi_vn(c0[4])
+            epi_rs(c0[4])
+            epi_sq(b0[3])
+            epi_u(c0[2])
+            nc.vector.reciprocal(out=small[:, 4:5], in_=small[:, 3:4])
+            epi_u(c0[3])
+            epi_sq(c0[1])
+            epi_r(c0[2])
+            epi_u(c0[4])
+            epi_r(c0[3])
+            epi_sq(c0[2])
+            epi_r(c0[4])
+            epi_sq(c0[3])
+            epi_sq(c0[4])
 
             tot = ps_tr.tile([P, 1], F32, name="tr")
-            for j in range(16):
-                nc.tensor.matmul(out=tot[:], lhsT=ones[:], rhs=stats[:, j : j + 1], start=(j == 0), stop=(j == 15))
+            n = len(stat_cols)
+            for j in range(n):
+                nc.tensor.matmul(out=tot[:], lhsT=ones[:], rhs=stats[:, j : j + 1], start=(j == 0), stop=(j == n - 1))
             nc.scalar.activation(out=small2[:, 0:1], in_=tot[:], func=ACT.Abs_reciprocal_sqrt, scale=small[:, 4:5])
-            for mm in range(NM):
-                nc.vector.scalar_tensor_tensor(out=r[:, mm, :], in0=r[:, mm, :], scalar=small2[:, 0:1], in1=w1t[:, mm, :], op0=ALU.mult, op1=ALU.add)
-                nc.sync.dma_start(out=out_v[:, mm, :], in_=r[:, mm, :])
+            cuts = [(0, 0, 256), (0, 256, 1024)] + [(mm, 0, 1024) for mm in range(1, NM)]
+            for mm, f0, f1 in cuts:
+                nc.vector.scalar_tensor_tensor(
+                    out=r[:, mm, f0:f1], in0=r[:, mm, f0:f1], scalar=small2[:, 0:1], in1=w1t[:, mm, f0:f1], op0=ALU.mult, op1=ALU.add
+                )
+                nc.sync.dma_start(out=out_v[:, mm, f0:f1], in_=r[:, mm, f0:f1])

@@ -30,10 +30,10 @@ C = -1.0 / 2**20
 A = (1.0 - 2.0 * C) / (2.0 * H)
 D_SCALE = -A / C
 CLAMP = 8.0
-DY_ON_V = {(g, c, b) for g in range(4) for c in range(2) for b in range(2) if (g, c) != (0, 1)}
+DY_ON_V = {(g, c, b) for g in range(4) for c in range(2) for b in range(2) if (g, c, b) not in ((0, 1, 0), (3, 0, 0))}
 XQ_POS = 1
 DYQ_LATE = 0
-X_PLAN = {(0, 0): "VV-1", (1, 0): "SP1", (2, 0): "SP2", (3, 0): "SP4", (0, 1): "SP6", (1, 1): "SV7", (2, 1): "SV8", (3, 1): "SP9"}
+X_PLAN = {(0, 0): "VV-1", (1, 0): "SP2", (2, 0): "SP2", (3, 0): "SP4", (0, 1): "SP6", (1, 1): "VV7", (2, 1): "SV8", (3, 1): "SV9"}
 
 G2_SCALE = C * math.sqrt(2.0 / 3.0 / T)
 M_SCALE = C * 2.0 / 3.0 / math.sqrt(T)
@@ -67,6 +67,7 @@ def tile_lambmlpbackwardstep_w8_kernel(tc, x_bytes, x_scale, a, dy, w2_words, w2
         stats = keep.tile([P, 2 * NM], F32, name="stats")
         small = keep.tile([P, 8], F32, name="small")
         small2 = keep.tile([P, 8], F32, name="small2")
+        small3 = keep.tile([P, 8], F32, name="small3")
 
         a_v = a.rearrange("(g p t) f -> g p t f", p=P, t=4)
         dy_v = dy.rearrange("(g p t) k -> g p t k", p=P, t=4)
@@ -120,25 +121,17 @@ def tile_lambmlpbackwardstep_w8_kernel(tc, x_bytes, x_scale, a, dy, w2_words, w2
 
         ac_tiles, g_tiles, da_tiles, vn_tiles = {}, {}, {}, {}
 
-        def clamp(i):
-            h, g, q = i // 8, (i // 2) % 4, i % 2
-            ac = sb.tile([P, 4, FS], BF16, name="ac", bufs=3)
-            ac_tiles[i] = ac
-            src = a_tiles[h, g][:, :, q * FS : (q + 1) * FS]
-            nc.vector.tensor_scalar(
-                out=ac[:],
-                in0=src,
-                scalar1=CLAMP,
-                scalar2=-CLAMP,
-                op0=ALU.min,
-                op1=ALU.max,
-            )
+        def clamp(j):
+            h, g = j // 4, j % 4
+            ac = sb.tile([P, 4, FH], BF16, name="ac", bufs=2)
+            ac_tiles[j] = ac
+            nc.vector.tensor_scalar(out=ac[:], in0=a_tiles[h, g][:], scalar1=CLAMP, scalar2=-CLAMP, op0=ALU.min, op1=ALU.max)
 
         def s_gelu(i):
-            src = ac_tiles[i][:].rearrange("p t f -> p (t f)")
-            gp = sb.tile([P, 4 * FS], F32, name="gp", bufs=2)
-            gm = sb.tile([P, 4 * FS], F32, name="gm", bufs=2)
-            th = sb.tile([P, 4 * FS], BF16, name="th", bufs=2)
+            src = ac_tiles[i // 2][:, :, (i % 2) * FS : (i % 2 + 1) * FS]
+            gp = sb.tile([P, 4, FS], F32, name="gp", bufs=2)
+            gm = sb.tile([P, 4, FS], F32, name="gm", bufs=2)
+            th = sb.tile([P, 4, FS], BF16, name="th", bufs=2)
             g_tiles[i] = (gp, gm, th)
             nc.scalar.activation(out=gp[:], in_=src, func=ACT.Gelu, scale=LAM, bias=H)
             nc.scalar.activation(out=gm[:], in_=src, func=ACT.Gelu, scale=LAM, bias=-H)
@@ -169,25 +162,26 @@ def tile_lambmlpbackwardstep_w8_kernel(tc, x_bytes, x_scale, a, dy, w2_words, w2
 
         def g_diff(i):
             gp, gm, th = g_tiles[i]
-            d = sb.tile([P, 4 * FS], F32, name="d", bufs=1)
+            d = sb.tile([P, 4, FS], F32, name="d", bufs=1)
             d_tiles[i] = d
             nc.gpsimd.tensor_tensor(out=d[:], in0=gm[:], in1=gp[:], op=ALU.subtract)
 
         def v_third(i):
             th = g_tiles[i][2]
-            q = sb.tile([P, 4 * FS], F32, name="q", bufs=1)
+            q = sb.tile([P, 4, FS], F32, name="q", bufs=1)
             q_tiles[i] = q
             nc.vector.scalar_tensor_tensor(out=q[:], in0=d_tiles[i][:], scalar=D_SCALE, in1=th[:], op0=ALU.mult, op1=ALU.add)
 
         def v_da(i, banks):
             q = q_tiles[i]
-            da = sb.tile([P, FS, 4], BF16, name="da", bufs=3, align_bytes=64)
-            da_tiles[i] = da
-            q_v = q[:].rearrange("p (t f) -> p f t", t=4)
+            if i % 2 == 0:
+                da_tiles[i // 2] = sb.tile([P, FH, 4], BF16, name="da", bufs=2, align_bytes=64)
+            da = da_tiles[i // 2]
+            q_v = q[:].rearrange("p t f -> p f t")
             for b in range(2):
                 fs = slice(b * P, (b + 1) * P)
                 nc.vector.scalar_tensor_tensor(
-                    out=da[:, fs, :],
+                    out=da[:, (i % 2) * FS + b * P : (i % 2) * FS + (b + 1) * P, :],
                     in0=q_v[:, fs, :],
                     scalar=1.0,
                     in1=banks[b][:].rearrange("p t f -> p f t"),
@@ -195,13 +189,13 @@ def tile_lambmlpbackwardstep_w8_kernel(tc, x_bytes, x_scale, a, dy, w2_words, w2
                     op1=ALU.mult,
                 )
 
-        def v_quant_da(i):
-            h, g, q = i // 8, (i // 2) % 4, i % 2
-            f0 = h * FH + q * FS
+        def v_quant_da(j):
+            h, g = j // 4, j % 4
+            fs = slice(h * FH, (h + 1) * FH)
             nc.vector.quantize_mx(
-                out=dac[:, g, f0 : f0 + FS].bitcast(X4),
-                scales=das[:, g, f0 : f0 + FS],
-                in_=da_tiles[i][:].rearrange("p f t -> p (f t)"),
+                out=dac[:, g, fs].bitcast(X4),
+                scales=das[:, g, fs],
+                in_=da_tiles[j][:].rearrange("p f t -> p (f t)"),
             )
 
         dyg_tiles = {}
@@ -236,7 +230,7 @@ def tile_lambmlpbackwardstep_w8_kernel(tc, x_bytes, x_scale, a, dy, w2_words, w2
         xw_tiles, xi_tiles = {}, {}
 
         def x_widen(g, e):
-            xw = sb.tile([P, 4, 512], BF16, name="xw", bufs=2)
+            xw = sb.tile([P, 4, 512], BF16, name="xw", bufs=2, align_bytes=64)
             xw_tiles[g, e] = xw
             for t in range(4):
                 src = x_tiles[g, e][:, t, :].bitcast(FP8)
@@ -306,7 +300,7 @@ def tile_lambmlpbackwardstep_w8_kernel(tc, x_bytes, x_scale, a, dy, w2_words, w2
                 vn = r[:, mm, FH:]
             else:
                 if mm % 2 == 0:
-                    vn_tiles["cur"] = sb.tile([P, 2, FH], F32, name="vn", bufs=3)
+                    vn_tiles["cur"] = sb.tile([P, 2, FH], F32, name="vn", tag="xw" if mm % 4 == 0 else "xi", bufs=2, align_bytes=64)
                 vn = vn_tiles["cur"][:, mm % 2, :]
             vn_tiles[h, mm] = vn_tiles.get("cur")
             gps_tiles[h, mm] = gps
@@ -337,16 +331,25 @@ def tile_lambmlpbackwardstep_w8_kernel(tc, x_bytes, x_scale, a, dy, w2_words, w2
             nc.vector.tensor_tensor(out=vn_of(blk), in0=mv_tiles[h, m0][1][:, m0 % 2 : m0 % 2 + n, :], in1=vn_of(blk), op=ALU.add)
 
         def epi_rs(blk):
-            nc.scalar.activation(out=vn_of(blk), in_=vn_of(blk), func=ACT.Abs_reciprocal_sqrt)
+            nc.scalar.activation(out=vn_of(blk), in_=vn_of(blk), func=ACT.Abs_reciprocal_sqrt, scale=W_SCALE * W_SCALE)
 
         def epi_u(blk):
             nc.vector.tensor_tensor(out=r_of(blk), in0=r_of(blk), in1=vn_of(blk), op=ALU.mult)
 
         def epi_r(blk):
             h, m0, n = blk
-            nc.vector.scalar_tensor_tensor(out=r_of(blk), in0=w1t[:, m0 : m0 + n, h * FH : (h + 1) * FH], scalar=-W_SCALE, in1=r_of(blk), op0=ALU.mult, op1=ALU.subtract)
+            nc.vector.scalar_tensor_tensor(out=r_of(blk), in0=w1t[:, m0 : m0 + n, h * FH : (h + 1) * FH], scalar=-1.0, in1=r_of(blk), op0=ALU.mult, op1=ALU.subtract)
 
         stat_cols = []
+
+        def epi_sum(mm):
+            bank = ps_tr.tile([P, FH], F32, name="tr")
+            nc.tensor.matmul(out=bank[:], lhsT=ident[:], rhs=r[:, mm, 0:FH], start=True, stop=False)
+            nc.tensor.matmul(out=bank[:], lhsT=identb[:], rhs=w1t[:, mm, 0:FH], start=False, stop=True)
+            junk = sb.tile([P, 2, FH], BF16, name="junk", bufs=1)
+            j = len(stat_cols)
+            stat_cols.append(mm)
+            nc.scalar.activation(out=junk[:, 0, :], in_=bank[:], func=ACT.Square, accum_out=stats[:, j : j + 1])
 
         def epi_sq(blk):
             h, m0, n = blk
@@ -402,7 +405,6 @@ def tile_lambmlpbackwardstep_w8_kernel(tc, x_bytes, x_scale, a, dy, w2_words, w2
             nc.vector.memset(small[:], 0.0)
             nc.scalar.activation(out=small[:, 0:1], in_=small[:, 1:2], func=ACT.Gelu)
             clamp(0)
-            clamp(1)
             s_gelu(0)
             x_widen(0, 0)
             for c in range(2):
@@ -437,10 +439,10 @@ def tile_lambmlpbackwardstep_w8_kernel(tc, x_bytes, x_scale, a, dy, w2_words, w2
                     x_widen(*unit)
                 if h == 0 and q == 0:
                     dy_quant(g, 1)
-                if i + 2 < 16:
-                    clamp(i + 2)
-                if i > 0:
-                    v_quant_da(i - 1)
+                if q == 0 and i + 2 < 16:
+                    clamp(i // 2 + 1)
+                if q == 0 and i > 0:
+                    v_quant_da(i // 2 - 1)
                 for unit in x_at.get((i, "iV"), []):
                     x_interleave(*unit)
                 for unit in x_at.get((i, "q"), []):
@@ -465,66 +467,72 @@ def tile_lambmlpbackwardstep_w8_kernel(tc, x_bytes, x_scale, a, dy, w2_words, w2
             c0 = [(1, 0, 2), (1, 2, 2), (1, 4, 2), (1, 6, 1), (1, 7, 1)]
             for k in range(3):
                 epi_rs(b0[k])
-            v_quant_da(15)
+            v_quant_da(7)
+
+            def front(mm):
+                epi_front(1, mm, *((ps_g, "gps") if mm % 2 == 0 else (ps_dh, "dh")))
+
+            front(0)
+            front(1)
             epi_vn(b0[3])
             epi_rs(b0[3])
             scr = sb.tile([P, P], F32, name="scr", bufs=1)
             nc.vector.tensor_tensor(out=scr[:], in0=gram[:], in1=ident[:], op=ALU.mult)
-            tail_pool = {0: (ps_g, "gps"), 1: (ps_dh, "dh")}
-
-            def front(mm):
-                epi_front(1, mm, *tail_pool[mm % 2])
-                epi_mn(1, mm)
-
             epi_u(b0[0])
             epi_u(b0[1])
-            front(0)
-            front(1)
-            epi_r(b0[0])
-            epi_sq(b0[0])
+            nc.vector.tensor_reduce(out=small[:, 2:3], in_=scr[:], op=ALU.add, axis=mybir.AxisListType.X)
+            epi_mn(1, 0)
+            front(2)
+            epi_mn(1, 1)
+            front(3)
+            epi_sum(0)
+            epi_sum(1)
+            epi_u(b0[2])
             epi_vn(c0[0])
             epi_rs(c0[0])
-            epi_r(b0[1])
-            epi_u(b0[2])
-            front(2)
-            front(3)
-            nc.vector.tensor_reduce(out=small[:, 2:3], in_=scr[:], op=ALU.add, axis=mybir.AxisListType.X)
-            epi_sq(b0[1])
-            epi_r(b0[2])
+            epi_mn(1, 2)
+            front(4)
+            epi_mn(1, 3)
+            front(5)
+            epi_sum(2)
+            epi_sum(3)
+            epi_u(b0[3])
             epi_vn(c0[1])
             epi_rs(c0[1])
+            epi_mn(1, 4)
+            front(6)
             epi_u(c0[0])
-            epi_u(b0[3])
-            front(4)
-            front(5)
-            epi_sq(b0[2])
-            tw = ps_tr.tile([P, 1], F32, name="tr")
-            nc.tensor.matmul(out=tw[:], lhsT=ones[:], rhs=small[:, 2:3], start=True, stop=True)
-            epi_r(c0[0])
+            epi_mn(1, 5)
+            front(7)
+            epi_sum(4)
+            epi_sum(5)
             epi_vn(c0[2])
             epi_rs(c0[2])
-            epi_r(b0[3])
-            nc.vector.tensor_scalar(out=small[:, 3:4], in0=tw[:], scalar1=0.25, scalar2=None, op0=ALU.mult)
-            epi_u(c0[1])
-            front(6)
-            front(7)
+            epi_r(c0[0])
             epi_sq(c0[0])
-            epi_r(c0[1])
+            epi_mn(1, 6)
+            epi_mn(1, 7)
+            epi_u(c0[1])
             epi_vn(c0[3])
             epi_rs(c0[3])
             epi_vn(c0[4])
             epi_rs(c0[4])
-            epi_sq(b0[3])
-            epi_u(c0[2])
-            nc.vector.reciprocal(out=small[:, 4:5], in_=small[:, 3:4])
-            epi_u(c0[3])
+            epi_sum(6)
+            epi_sum(7)
+            epi_r(c0[1])
             epi_sq(c0[1])
+            tw = ps_tr.tile([P, 1], F32, name="tr")
+            nc.tensor.matmul(out=tw[:], lhsT=ones[:], rhs=small[:, 2:3], start=True, stop=True)
+            epi_u(c0[2])
+            nc.vector.tensor_scalar(out=small[:, 3:4], in0=tw[:], scalar1=0.25, scalar2=None, op0=ALU.mult)
+            epi_u(c0[3])
             epi_r(c0[2])
+            epi_sq(c0[2])
+            nc.vector.reciprocal(out=small[:, 4:5], in_=small[:, 3:4])
             epi_u(c0[4])
             epi_r(c0[3])
-            epi_sq(c0[2])
-            epi_r(c0[4])
             epi_sq(c0[3])
+            epi_r(c0[4])
             epi_sq(c0[4])
 
             tot = ps_tr.tile([P, 1], F32, name="tr")
@@ -532,9 +540,27 @@ def tile_lambmlpbackwardstep_w8_kernel(tc, x_bytes, x_scale, a, dy, w2_words, w2
             for j in range(n):
                 nc.tensor.matmul(out=tot[:], lhsT=ones[:], rhs=stats[:, j : j + 1], start=(j == 0), stop=(j == n - 1))
             nc.scalar.activation(out=small2[:, 0:1], in_=tot[:], func=ACT.Abs_reciprocal_sqrt, scale=small[:, 4:5])
-            cuts = [(0, 0, 256), (0, 256, 1024)] + [(mm, 0, 1024) for mm in range(1, NM)]
-            for mm, f0, f1 in cuts:
+            coef = small2[:, 0:1]
+            nc.vector.tensor_scalar(out=small3[:, 0:1], in0=coef, scalar1=-1.0, scalar2=1.0, op0=ALU.mult, op1=ALU.add)
+            nc.vector.tensor_scalar(out=small3[:, 1:2], in0=coef, scalar1=-1.0, scalar2=None, op0=ALU.mult)
+            wk_tiles = []
+            for k in range(4):
+                wk = sb.tile([P, 2, FH], F32, name="wk", tag="gp" if k < 2 else "gm", bufs=2)
+                wk_tiles.append(wk)
+                nc.scalar.activation(out=wk[:], in_=w1t[:, 2 * k : 2 * k + 2, 0:FH], func=ACT.Copy, scale=small3[:, 0:1])
+
+            def finish(h, m0, n):
+                blk = (h, m0, n)
+                fs = slice(h * FH, (h + 1) * FH)
                 nc.vector.scalar_tensor_tensor(
-                    out=r[:, mm, f0:f1], in0=r[:, mm, f0:f1], scalar=small2[:, 0:1], in1=w1t[:, mm, f0:f1], op0=ALU.mult, op1=ALU.add
+                    out=r_of(blk),
+                    in0=r_of(blk),
+                    scalar=coef if h else small3[:, 1:2],
+                    in1=w1t[:, m0 : m0 + n, fs] if h else wk_tiles[m0 // 2][:],
+                    op0=ALU.mult,
+                    op1=ALU.add,
                 )
-                nc.sync.dma_start(out=out_v[:, mm, f0:f1], in_=r[:, mm, f0:f1])
+                nc.sync.dma_start(out=out_v[:, m0 : m0 + n, fs], in_=r_of(blk))
+
+            for blk in [(1, 0, 1), (1, 1, 1), (1, 2, 2), (0, 0, 2), (1, 4, 2), (0, 2, 2), (1, 6, 2), (0, 4, 2), (0, 6, 2)]:
+                finish(*blk)

@@ -33,7 +33,11 @@ CLAMP = 8.0
 DY_ON_V = {(g, c, b) for g in range(4) for c in range(2) for b in range(2) if (g, c, b) not in ((0, 1, 0), (3, 0, 0))}
 XQ_POS = 1
 DYQ_LATE = 0
-X_PLAN = {(0, 0): "VV-1", (1, 0): "SP2", (2, 0): "SP2", (3, 0): "SP4", (0, 1): "SP6", (1, 1): "VV7", (2, 1): "SV8", (3, 1): "SV9"}
+DH_FIRST = 0
+X_FIRST = 1
+X_LAG = 1
+DY_LEAD = 0
+X_PLAN = {(0, 0): "VV-1", (1, 0): "SV1", (2, 0): "SP2", (3, 0): "SP4", (0, 1): "SV4", (1, 1): "SP6", (2, 1): "SV7", (3, 1): "SV8"}
 
 G2_SCALE = C * math.sqrt(2.0 / 3.0 / T)
 M_SCALE = C * 2.0 / 3.0 / math.sqrt(T)
@@ -45,10 +49,9 @@ def tile_lambmlpbackwardstep_w8_kernel(tc, x_bytes, x_scale, a, dy, w2_words, w2
     with ExitStack() as ctx:
         keep = ctx.enter_context(tc.tile_pool(name="keep", bufs=1))
         sb = ctx.enter_context(tc.tile_pool(name="sb", bufs=2))
-        ps_dh = ctx.enter_context(tc.psum_pool(name="ps_dh", bufs=3))
+        ps_dh = ctx.enter_context(tc.psum_pool(name="ps_dh", bufs=4))
         ps_tr = ctx.enter_context(tc.psum_pool(name="ps_tr", bufs=2))
         ps_g = ctx.enter_context(tc.psum_pool(name="ps_g", bufs=2))
-        ps_w = ctx.enter_context(tc.psum_pool(name="ps_w", bufs=1))
 
         ident = keep.tile([P, P], F32, name="ident")
         identb = keep.tile([P, P], BF16, name="identb")
@@ -67,7 +70,6 @@ def tile_lambmlpbackwardstep_w8_kernel(tc, x_bytes, x_scale, a, dy, w2_words, w2
         stats = keep.tile([P, 2 * NM], F32, name="stats")
         small = keep.tile([P, 8], F32, name="small")
         small2 = keep.tile([P, 8], F32, name="small2")
-        small3 = keep.tile([P, 8], F32, name="small3")
 
         a_v = a.rearrange("(g p t) f -> g p t f", p=P, t=4)
         dy_v = dy.rearrange("(g p t) k -> g p t k", p=P, t=4)
@@ -342,15 +344,6 @@ def tile_lambmlpbackwardstep_w8_kernel(tc, x_bytes, x_scale, a, dy, w2_words, w2
 
         stat_cols = []
 
-        def epi_sum(mm):
-            bank = ps_tr.tile([P, FH], F32, name="tr")
-            nc.tensor.matmul(out=bank[:], lhsT=ident[:], rhs=r[:, mm, 0:FH], start=True, stop=False)
-            nc.tensor.matmul(out=bank[:], lhsT=identb[:], rhs=w1t[:, mm, 0:FH], start=False, stop=True)
-            junk = sb.tile([P, 2, FH], BF16, name="junk", bufs=1)
-            j = len(stat_cols)
-            stat_cols.append(mm)
-            nc.scalar.activation(out=junk[:, 0, :], in_=bank[:], func=ACT.Square, accum_out=stats[:, j : j + 1])
-
         def epi_sq(blk):
             h, m0, n = blk
             junk = sb.tile([P, 2, FH], BF16, name="junk", bufs=1)
@@ -358,12 +351,14 @@ def tile_lambmlpbackwardstep_w8_kernel(tc, x_bytes, x_scale, a, dy, w2_words, w2
             stat_cols.append(blk)
             nc.scalar.activation(out=junk[:, 0:n, :], in_=r_of(blk), func=ACT.Square, accum_out=stats[:, j : j + 1])
 
-        gram = ps_w.tile([P, P], F32, name="gram")
 
-        def w_gram(mm):
-            for b in range(8):
-                blk = w1t[:, mm, b * P : (b + 1) * P]
-                nc.tensor.matmul(out=gram[:], lhsT=blk, rhs=blk, start=(mm == 0 and b == 0), stop=(mm == NM - 1 and b == 7))
+        def w_gram():
+            gram = ps_dh.tile([P, P], F32, name="dh")
+            for mm in range(NM):
+                for b in range(8):
+                    blk = w1t[:, mm, b * P : (b + 1) * P]
+                    nc.tensor.matmul(out=gram[:], lhsT=blk, rhs=blk, start=(mm == 0 and b == 0), stop=(mm == NM - 1 and b == 7))
+            return gram
 
         with tc.manual_schedule():
             load_a(0, 0)
@@ -404,65 +399,83 @@ def tile_lambmlpbackwardstep_w8_kernel(tc, x_bytes, x_scale, a, dy, w2_words, w2
 
             nc.vector.memset(small[:], 0.0)
             nc.scalar.activation(out=small[:, 0:1], in_=small[:, 1:2], func=ACT.Gelu)
+            def dy_unit(k):
+                return k // 2, k % 2
+
             clamp(0)
             s_gelu(0)
             x_widen(0, 0)
-            for c in range(2):
-                dy_transpose(0, c)
-                dy_copy(0, c, 0)
-                dy_copy(0, c, 1)
-            dy_quant(0, 0)
+            for k in range(2 + DY_LEAD):
+                dy_transpose(*dy_unit(k))
+                dy_copy(*dy_unit(k), 0)
+                dy_copy(*dy_unit(k), 1)
+                if k == 1:
+                    dy_quant(0, 0)
+                    x_interleave(0, 0)
+                    dy_quant(0, 1)
+                    x_quant(0, 0)
+            if DY_LEAD:
+                dy_transpose(1, 1)
             x_at = {}
             for unit, plan in X_PLAN.items():
+                if unit == (0, 0):
+                    continue
                 step = int(plan[2:])
-                if unit != (0, 0):
-                    x_at.setdefault((step, "w"), []).append(unit)
-                x_at.setdefault((step + 1, "i" + plan[1]), []).append(unit)
-                x_at.setdefault((step + 2, "q"), []).append(unit)
+                x_at.setdefault((step, "w"), []).append(unit)
+                if plan[1] == "P":
+                    x_at.setdefault((step + 1, "t"), []).append(unit)
+                    x_at.setdefault((step + 1 + X_LAG, "c"), []).append(unit)
+                    x_at.setdefault((step + 2 + (X_LAG > 0), "q"), []).append(unit)
+                else:
+                    x_at.setdefault((step + 1, "v"), []).append(unit)
+                    x_at.setdefault((step + 2, "q"), []).append(unit)
 
             for i in range(16):
                 h, g, q = i // 8, (i // 2) % 4, i % 2
-                nxt = h == 0 and g < 3
-                for unit in x_at.get((i, "iP"), []):
-                    x_transfer(*unit)
+                if X_FIRST:
+                    for unit in x_at.get((i, "t"), []):
+                        x_transfer(*unit)
                 if i > 0:
                     s_gelu(i)
                 g_diff(i)
-                if nxt:
-                    dy_transpose(g + 1, q)
-                    for b in range(2):
-                        if (g + 1, q, b) not in DY_ON_V:
-                            dy_copy(g + 1, q, b)
-                for unit in x_at.get((i, "iP"), []):
+                for unit in x_at.get((i, "c"), []):
                     x_interleave(*unit)
                 for unit in x_at.get((i, "w"), []):
                     x_widen(*unit)
-                if h == 0 and q == 0:
-                    dy_quant(g, 1)
+                kq = i + 1 + DY_LEAD
+                if 2 <= kq < 8:
+                    dy_quant(*dy_unit(kq))
                 if q == 0 and i + 2 < 16:
                     clamp(i // 2 + 1)
                 if q == 0 and i > 0:
                     v_quant_da(i // 2 - 1)
-                for unit in x_at.get((i, "iV"), []):
-                    x_interleave(*unit)
                 for unit in x_at.get((i, "q"), []):
                     x_quant(*unit)
-                if nxt and q == 1:
-                    dy_quant(g + 1, 0)
+                for unit in x_at.get((i, "v"), []):
+                    x_interleave(*unit)
                 if i in (11, 13, 15):
                     epi_vn((0, i - 11, 2))
                 v_third(i)
+                kc = i + 2 + DY_LEAD
+                kt = i + 2 + 2 * DY_LEAD
+                if DH_FIRST:
+                    banks = pe_dh(i)
+                if kt < 8:
+                    dy_transpose(*dy_unit(kt))
                 if h == 1:
                     epi_front(0, i - 8)
-                banks = pe_dh(i)
-                if nxt and (g + 1, q, 0) in DY_ON_V:
-                    dy_copy(g + 1, q, 0)
+                if not DH_FIRST:
+                    banks = pe_dh(i)
+                if not X_FIRST:
+                    for unit in x_at.get((i, "t"), []):
+                        x_transfer(*unit)
+                if kc < 8:
+                    dy_copy(*dy_unit(kc), 0)
                 if h == 1:
                     epi_mn(0, i - 8)
-                    w_gram(i - 8)
                 v_da(i, banks)
-                if nxt and (g + 1, q, 1) in DY_ON_V:
-                    dy_copy(g + 1, q, 1)
+                if kc < 8:
+                    dy_copy(*dy_unit(kc), 1)
             b0 = [(0, 2 * k, 2) for k in range(4)]
             c0 = [(1, 0, 2), (1, 2, 2), (1, 4, 2), (1, 6, 1), (1, 7, 1)]
             for k in range(3):
@@ -474,64 +487,65 @@ def tile_lambmlpbackwardstep_w8_kernel(tc, x_bytes, x_scale, a, dy, w2_words, w2
 
             front(0)
             front(1)
+            epi_u(b0[0])
             epi_vn(b0[3])
             epi_rs(b0[3])
-            scr = sb.tile([P, P], F32, name="scr", bufs=1)
-            nc.vector.tensor_tensor(out=scr[:], in0=gram[:], in1=ident[:], op=ALU.mult)
-            epi_u(b0[0])
             epi_u(b0[1])
-            nc.vector.tensor_reduce(out=small[:, 2:3], in_=scr[:], op=ALU.add, axis=mybir.AxisListType.X)
+            epi_r(b0[0])
+            epi_sq(b0[0])
             epi_mn(1, 0)
             front(2)
             epi_mn(1, 1)
             front(3)
-            epi_sum(0)
-            epi_sum(1)
             epi_u(b0[2])
+            epi_r(b0[1])
             epi_vn(c0[0])
             epi_rs(c0[0])
+            epi_sq(b0[1])
             epi_mn(1, 2)
             front(4)
             epi_mn(1, 3)
             front(5)
-            epi_sum(2)
-            epi_sum(3)
             epi_u(b0[3])
+            epi_r(b0[2])
             epi_vn(c0[1])
             epi_rs(c0[1])
+            epi_sq(b0[2])
             epi_mn(1, 4)
             front(6)
             epi_u(c0[0])
             epi_mn(1, 5)
             front(7)
-            epi_sum(4)
-            epi_sum(5)
+            gram = w_gram()
+            epi_r(b0[3])
             epi_vn(c0[2])
             epi_rs(c0[2])
+            epi_sq(b0[3])
             epi_r(c0[0])
-            epi_sq(c0[0])
             epi_mn(1, 6)
             epi_mn(1, 7)
+            epi_sq(c0[0])
             epi_u(c0[1])
             epi_vn(c0[3])
             epi_rs(c0[3])
             epi_vn(c0[4])
             epi_rs(c0[4])
-            epi_sum(6)
-            epi_sum(7)
             epi_r(c0[1])
             epi_sq(c0[1])
+            scr = sb.tile([P, P], F32, name="scr", bufs=1)
+            nc.vector.tensor_tensor(out=scr[:], in0=gram[:], in1=ident[:], op=ALU.mult)
+            epi_u(c0[2])
+            nc.vector.tensor_reduce(out=small[:, 2:3], in_=scr[:], op=ALU.add, axis=mybir.AxisListType.X)
             tw = ps_tr.tile([P, 1], F32, name="tr")
             nc.tensor.matmul(out=tw[:], lhsT=ones[:], rhs=small[:, 2:3], start=True, stop=True)
-            epi_u(c0[2])
-            nc.vector.tensor_scalar(out=small[:, 3:4], in0=tw[:], scalar1=0.25, scalar2=None, op0=ALU.mult)
             epi_u(c0[3])
             epi_r(c0[2])
             epi_sq(c0[2])
-            nc.vector.reciprocal(out=small[:, 4:5], in_=small[:, 3:4])
+            nc.vector.tensor_scalar(out=small[:, 3:4], in0=tw[:], scalar1=0.25, scalar2=None, op0=ALU.mult)
             epi_u(c0[4])
             epi_r(c0[3])
             epi_sq(c0[3])
+            nc.vector.reciprocal(out=small[:, 4:5], in_=small[:, 3:4])
             epi_r(c0[4])
             epi_sq(c0[4])
 
@@ -540,27 +554,8 @@ def tile_lambmlpbackwardstep_w8_kernel(tc, x_bytes, x_scale, a, dy, w2_words, w2
             for j in range(n):
                 nc.tensor.matmul(out=tot[:], lhsT=ones[:], rhs=stats[:, j : j + 1], start=(j == 0), stop=(j == n - 1))
             nc.scalar.activation(out=small2[:, 0:1], in_=tot[:], func=ACT.Abs_reciprocal_sqrt, scale=small[:, 4:5])
-            coef = small2[:, 0:1]
-            nc.vector.tensor_scalar(out=small3[:, 0:1], in0=coef, scalar1=-1.0, scalar2=1.0, op0=ALU.mult, op1=ALU.add)
-            nc.vector.tensor_scalar(out=small3[:, 1:2], in0=coef, scalar1=-1.0, scalar2=None, op0=ALU.mult)
-            wk_tiles = []
-            for k in range(4):
-                wk = sb.tile([P, 2, FH], F32, name="wk", tag="gp" if k < 2 else "gm", bufs=2)
-                wk_tiles.append(wk)
-                nc.scalar.activation(out=wk[:], in_=w1t[:, 2 * k : 2 * k + 2, 0:FH], func=ACT.Copy, scale=small3[:, 0:1])
-
-            def finish(h, m0, n):
-                blk = (h, m0, n)
-                fs = slice(h * FH, (h + 1) * FH)
+            for mm, f0, f1 in [(0, 0, 256), (0, 256, 1024)] + [(mm, 0, 1024) for mm in range(1, NM)]:
                 nc.vector.scalar_tensor_tensor(
-                    out=r_of(blk),
-                    in0=r_of(blk),
-                    scalar=coef if h else small3[:, 1:2],
-                    in1=w1t[:, m0 : m0 + n, fs] if h else wk_tiles[m0 // 2][:],
-                    op0=ALU.mult,
-                    op1=ALU.add,
+                    out=r[:, mm, f0:f1], in0=r[:, mm, f0:f1], scalar=small2[:, 0:1], in1=w1t[:, mm, f0:f1], op0=ALU.mult, op1=ALU.add
                 )
-                nc.sync.dma_start(out=out_v[:, m0 : m0 + n, fs], in_=r_of(blk))
-
-            for blk in [(1, 0, 1), (1, 1, 1), (1, 2, 2), (0, 0, 2), (1, 4, 2), (0, 2, 2), (1, 6, 2), (0, 4, 2), (0, 6, 2)]:
-                finish(*blk)
+                nc.sync.dma_start(out=out_v[:, mm, f0:f1], in_=r[:, mm, f0:f1])

import math
from contextlib import ExitStack

import concourse.mybir as mybir
from concourse.masks import make_identity

T, D, F = 2048, 1024, 1024
FLOPS = 2 * T * D * F * 2

F32 = mybir.dt.float32
BF16 = mybir.dt.bfloat16
U32 = mybir.dt.uint32
U8 = mybir.dt.uint8
I32 = mybir.dt.int32
FP8 = mybir.dt.float8_e4m3fn
X4 = mybir.dt.float8_e4m3fn_x4
ALU = mybir.AluOpType
ACT = mybir.ActivationFunctionType

P = 128
NG = 4
NM = 8
FH = 512
FS = 256

LAM = 1.0 + 9.0 / 2**23
H = 2568.0 / 2**20
NU = 211.0 / 256
C = -1.0 / 2**20
A = (1.0 - 2.0 * C) / (2.0 * H)
D_SCALE = -A / C
CLAMP = 8.0
DY_ON_V = {(g, c, b) for g in range(4) for c in range(2) for b in range(2) if (g, c, b) not in ((0, 1, 0), (3, 0, 0))}
XQ_POS = 1
DYQ_LATE = 0
DH_FIRST = 0
X_FIRST = 1
X_LAG = 1
DY_LEAD = 0
X_PLAN = {(0, 0): "VV-1", (1, 0): "SV1", (2, 0): "SP2", (3, 0): "SP4", (0, 1): "SV4", (1, 1): "SP6", (2, 1): "SV7", (3, 1): "SV8"}

G2_SCALE = C * math.sqrt(2.0 / 3.0 / T)
M_SCALE = C * 2.0 / 3.0 / math.sqrt(T)
W_SCALE = 0.1 / math.sqrt(0.6)


def tile_lambmlpbackwardstep_w8_kernel(tc, x_bytes, x_scale, a, dy, w2_words, w2_scales, w1, m, v, out):
    nc = tc.nc
    with ExitStack() as ctx:
        keep = ctx.enter_context(tc.tile_pool(name="keep", bufs=1))
        sb = ctx.enter_context(tc.tile_pool(name="sb", bufs=2))
        ps_dh = ctx.enter_context(tc.psum_pool(name="ps_dh", bufs=4))
        ps_tr = ctx.enter_context(tc.psum_pool(name="ps_tr", bufs=2))
        ps_g = ctx.enter_context(tc.psum_pool(name="ps_g", bufs=2))

        ident = keep.tile([P, P], F32, name="ident")
        identb = keep.tile([P, P], BF16, name="identb")
        ones = keep.tile([P, P], F32, name="ones")
        xs = keep.tile([P, NG, 4], F32, name="xs")
        dyc = keep.tile([P, 2, T], U32, name="dyc", align_bytes=64)
        dys = keep.tile([P, 2, T], U8, name="dys", align_bytes=64)
        wc = keep.tile([P, 2, F], U32, name="wc", align_bytes=64)
        ws = keep.tile([P, 2, F], U8, name="ws", align_bytes=64)
        xc = keep.tile([P, NG, D], U32, name="xc", align_bytes=64)
        xsc = keep.tile([P, NG, D], U8, name="xsc", align_bytes=64)
        dac = keep.tile([P, NG, F], U32, name="dac", align_bytes=64)
        das = keep.tile([P, NG, F], U8, name="das", align_bytes=64)
        w1t = keep.tile([P, NM, F], BF16, name="w1t")
        r = keep.tile([P, NM, F], F32, name="r")
        stats = keep.tile([P, 2 * NM], F32, name="stats")
        small = keep.tile([P, 8], F32, name="small")
        small2 = keep.tile([P, 8], F32, name="small2")

        a_v = a.rearrange("(g p t) f -> g p t f", p=P, t=4)
        dy_v = dy.rearrange("(g p t) k -> g p t k", p=P, t=4)
        x_v = x_bytes.rearrange("(g p t) d -> g p t d", p=P, t=4)
        xs_v = x_scale.rearrange("(g p t) o -> p g (t o)", p=P, t=4)
        w1_v = w1.rearrange("(m p) f -> p m f", p=P)
        m_v = m.rearrange("(m p) f -> p m f", p=P)
        v_v = v.rearrange("(m p) f -> p m f", p=P)
        out_v = out.rearrange("(m p) f -> p m f", p=P)

        nc.gpsimd.memset(ws[:].rearrange("p c n -> p (c n)").bitcast(I32), 0)
        make_identity(nc, ident[:])
        make_identity(nc, identb[:])
        nc.gpsimd.memset(ones[:], 1.0)

        a_tiles, dy_tiles, x_tiles, mv_tiles = {}, {}, {}, {}

        def load_a(h, g):
            t = sb.tile([P, 4, FH], BF16, name="at", bufs=2)
            a_tiles[h, g] = t
            parts = 2 if (h, g) == (0, 0) else 1
            w = FH // parts
            for i in range(parts):
                nc.sync.dma_start(out=t[:, :, i * w : (i + 1) * w], in_=a_v[g][:, :, h * FH + i * w : h * FH + (i + 1) * w])

        def load_dy(g):
            t = sb.tile([P, 4, D], BF16, name="dyt", bufs=2)
            dy_tiles[g] = t
            parts = 2 if g == 0 else 1
            w = D // parts
            for i in range(parts):
                nc.sync.dma_start(out=t[:, :, i * w : (i + 1) * w], in_=dy_v[g][:, :, i * w : (i + 1) * w])

        def load_x(g, e):
            t = sb.tile([P, 4, 512], U8, name="xb", bufs=3)
            x_tiles[g, e] = t
            nc.sync.dma_start(out=t[:], in_=x_v[g][:, :, e * 512 : (e + 1) * 512])

        def load_w(h):
            for c in range(2):
                src = w2_words[c].rearrange("p n t -> p (n t)")[:, 4 * h * FH : 4 * (h + 1) * FH]
                nc.sync.dma_start(out=wc[:, c, h * FH : (h + 1) * FH].bitcast(I32), in_=src.bitcast(I32))

        def load_mv(h, k):
            mt = sb.tile([P, 2, FH], BF16, name="mt", bufs=2)
            vt = sb.tile([P, 2, FH], BF16, name="vt", bufs=3)
            for mm in (2 * k, 2 * k + 1):
                mv_tiles[h, mm] = (mt, vt)
            nc.sync.dma_start(out=mt[:], in_=m_v[:, 2 * k : 2 * k + 2, h * FH : (h + 1) * FH])
            nc.sync.dma_start(out=vt[:], in_=v_v[:, 2 * k : 2 * k + 2, h * FH : (h + 1) * FH])

        ac_tiles, g_tiles, da_tiles, vn_tiles = {}, {}, {}, {}

        def clamp(j):
            h, g = j // 4, j % 4
            ac = sb.tile([P, 4, FH], BF16, name="ac", bufs=2)
            ac_tiles[j] = ac
            nc.vector.tensor_scalar(out=ac[:], in0=a_tiles[h, g][:], scalar1=CLAMP, scalar2=-CLAMP, op0=ALU.min, op1=ALU.max)

        def s_gelu(i):
            src = ac_tiles[i // 2][:, :, (i % 2) * FS : (i % 2 + 1) * FS]
            gp = sb.tile([P, 4, FS], F32, name="gp", bufs=2)
            gm = sb.tile([P, 4, FS], F32, name="gm", bufs=2)
            th = sb.tile([P, 4, FS], BF16, name="th", bufs=2)
            g_tiles[i] = (gp, gm, th)
            nc.scalar.activation(out=gp[:], in_=src, func=ACT.Gelu, scale=LAM, bias=H)
            nc.scalar.activation(out=gm[:], in_=src, func=ACT.Gelu, scale=LAM, bias=-H)
            nc.scalar.activation(out=th[:], in_=src, func=ACT.Tanh, scale=NU)

        def pe_dh(i):
            h, g, q = i // 8, (i // 2) % 4, i % 2
            banks = []
            for b in range(2):
                dh = ps_dh.tile([P, 4, P], F32, name="dh")
                banks.append(dh)
                f0 = h * FH + q * FS + b * P
                for t in range(4):
                    t0 = g * 512 + t * P
                    for c in range(2):
                        nc.tensor.matmul_mx(
                            out=dh[:, t, :],
                            lhsT=dyc[:, c, t0 : t0 + P].bitcast(X4),
                            lhsT_scale=dys[:, c, t0 : t0 + P],
                            rhs=wc[:, c, f0 : f0 + P].bitcast(X4),
                            rhs_scale=ws[:, c, f0 : f0 + P],
                            start=(c == 0),
                            stop=(c == 1),
                        )
            return banks

        d_tiles, q_tiles = {}, {}

        def g_diff(i):
            gp, gm, th = g_tiles[i]
            d = sb.tile([P, 4, FS], F32, name="d", bufs=1)
            d_tiles[i] = d
            nc.gpsimd.tensor_tensor(out=d[:], in0=gm[:], in1=gp[:], op=ALU.subtract)

        def v_third(i):
            th = g_tiles[i][2]
            q = sb.tile([P, 4, FS], F32, name="q", bufs=1)
            q_tiles[i] = q
            nc.vector.scalar_tensor_tensor(out=q[:], in0=d_tiles[i][:], scalar=D_SCALE, in1=th[:], op0=ALU.mult, op1=ALU.add)

        def v_da(i, banks):
            q = q_tiles[i]
            if i % 2 == 0:
                da_tiles[i // 2] = sb.tile([P, FH, 4], BF16, name="da", bufs=2, align_bytes=64)
            da = da_tiles[i // 2]
            q_v = q[:].rearrange("p t f -> p f t")
            for b in range(2):
                fs = slice(b * P, (b + 1) * P)
                nc.vector.scalar_tensor_tensor(
                    out=da[:, (i % 2) * FS + b * P : (i % 2) * FS + (b + 1) * P, :],
                    in0=q_v[:, fs, :],
                    scalar=1.0,
                    in1=banks[b][:].rearrange("p t f -> p f t"),
                    op0=ALU.add,
                    op1=ALU.mult,
                )

        def v_quant_da(j):
            h, g = j // 4, j % 4
            fs = slice(h * FH, (h + 1) * FH)
            nc.vector.quantize_mx(
                out=dac[:, g, fs].bitcast(X4),
                scales=das[:, g, fs],
                in_=da_tiles[j][:].rearrange("p f t -> p (f t)"),
            )

        dyg_tiles = {}

        dy_banks = {}

        def dy_transpose(g, c):
            words = dy_tiles[g][:].bitcast(F32)
            dyg_tiles[g, c] = sb.tile([P, 512, 4], BF16, name="dyg", bufs=2, align_bytes=64)
            for b in range(2):
                tr = ps_tr.tile([P, 2, 2, P], F32, name="tr")
                dy_banks[g, c, b] = tr
                for tt in range(2):
                    for u in range(2):
                        nc.tensor.transpose(tr[:, tt, u, :], words[:, 2 * b + tt, 256 * c + u : 256 * (c + 1) : 2], ident[:])

        def dy_copy(g, c, b):
            dst = dyg_tiles[g, c][:].rearrange("p n e -> p (n e)").bitcast(F32)
            copy = nc.vector.tensor_copy if (g, c, b) in DY_ON_V else nc.scalar.copy
            copy(
                out=dst[:, b * 512 : (b + 1) * 512].rearrange("p (t m u) -> p t m u", t=2, u=2),
                in_=dy_banks[g, c, b][:].rearrange("p t u m -> p t m u"),
            )

        def dy_quant(g, c):
            nc.vector.quantize_mx(
                out=dyc[:, c, g * 512 : (g + 1) * 512].bitcast(X4),
                scales=dys[:, c, g * 512 : (g + 1) * 512],
                in_=dyg_tiles[g, c][:].rearrange("p n e -> p (n e)"),
            )

        xw_tiles, xi_tiles = {}, {}

        def x_widen(g, e):
            xw = sb.tile([P, 4, 512], BF16, name="xw", bufs=2, align_bytes=64)
            xw_tiles[g, e] = xw
            for t in range(4):
                src = x_tiles[g, e][:, t, :].bitcast(FP8)
                if X_PLAN[g, e][0] == "V":
                    nc.vector.tensor_scalar(out=xw[:, t, :], in0=src, scalar1=xs[:, g, t : t + 1], scalar2=None, op0=ALU.mult)
                else:
                    nc.scalar.activation(out=xw[:, t, :], in_=src, func=ACT.Copy, scale=xs[:, g, t : t + 1])

        x_banks = {}

        def x_transfer(g, e):
            banks = []
            for b in range(2):
                bank = (ps_g if e == 0 else ps_tr).tile([P, 2, P, 4], BF16, name="gps" if e == 0 else "tr")
                banks.append(bank)
                for j in range(2):
                    d0 = (2 * b + j) * P
                    nc.tensor.matmul(
                        out=bank[:, j, :, :].rearrange("p d t -> p (d t)"),
                        lhsT=identb[:],
                        rhs=xw_tiles[g, e][:, :, d0 : d0 + P].rearrange("p t d -> p d t"),
                        start=True,
                        stop=True,
                    )
            x_banks[g, e] = banks

        def x_interleave(g, e):
            xi = sb.tile([P, 512, 4], BF16, name="xi", bufs=2, align_bytes=64)
            xi_tiles[g, e] = xi
            if X_PLAN[g, e][1] == "V":
                nc.vector.tensor_copy(
                    out=xi[:].rearrange("p (c i) t -> p c t i", i=4),
                    in_=xw_tiles[g, e][:].rearrange("p t (c i) -> p c t i", i=4),
                )
                return
            for b in range(2):
                nc.scalar.copy(
                    out=xi[:, b * 256 : (b + 1) * 256, :].rearrange("p d t -> p (d t)"),
                    in_=x_banks[g, e][b][:].rearrange("p j d t -> p (j d t)"),
                )

        def x_quant(g, e):
            nc.vector.quantize_mx(
                out=xc[:, g, e * 512 : (e + 1) * 512].bitcast(X4),
                scales=xsc[:, g, e * 512 : (e + 1) * 512],
                in_=xi_tiles[g, e][:].rearrange("p n t -> p (n t)"),
            )

        gps_tiles = {}
        vn_dst = {}

        def epi_front(h, mm, pool=None, name="gps", sq=True):
            fs = slice(h * FH, (h + 1) * FH)
            ms = slice(mm * P, (mm + 1) * P)
            gps = (pool or ps_g).tile([P, FH], F32, name=name)
            for g in range(NG):
                nc.tensor.matmul_mx(
                    out=gps[:],
                    lhsT=xc[:, g, ms].bitcast(X4),
                    lhsT_scale=xsc[:, g, ms],
                    rhs=dac[:, g, fs].bitcast(X4),
                    rhs_scale=das[:, g, fs],
                    start=(g == 0),
                    stop=(g == NG - 1),
                )
            if h == 0:
                vn = r[:, mm, FH:]
            else:
                if mm % 2 == 0:
                    vn_tiles["cur"] = sb.tile([P, 2, FH], F32, name="vn", tag="xw" if mm % 4 == 0 else "xi", bufs=2, align_bytes=64)
                vn = vn_tiles["cur"][:, mm % 2, :]
            vn_tiles[h, mm] = vn_tiles.get("cur")
            gps_tiles[h, mm] = gps
            vn_dst[h, mm] = vn
            if sq:
                epi_g2(h, mm)

        def epi_g2(h, mm):
            nc.scalar.activation(out=vn_dst[h, mm], in_=gps_tiles[h, mm][:], func=ACT.Square, scale=G2_SCALE)

        def epi_mn(h, mm):
            gps = gps_tiles[h, mm]
            fs = slice(h * FH, (h + 1) * FH)
            nc.vector.scalar_tensor_tensor(out=r[:, mm, fs], in0=gps[:], scalar=M_SCALE, in1=mv_tiles[h, mm][0][:, mm % 2, :], op0=ALU.mult, op1=ALU.add)

        def vn_of(blk):
            h, m0, n = blk
            if h == 0:
                return r[:, m0 : m0 + n, FH:]
            return vn_tiles[h, m0][:, m0 % 2 : m0 % 2 + n, :]

        def r_of(blk):
            h, m0, n = blk
            return r[:, m0 : m0 + n, h * FH : (h + 1) * FH]

        def epi_vn(blk):
            h, m0, n = blk
            nc.vector.tensor_tensor(out=vn_of(blk), in0=mv_tiles[h, m0][1][:, m0 % 2 : m0 % 2 + n, :], in1=vn_of(blk), op=ALU.add)

        def epi_rs(blk):
            nc.scalar.activation(out=vn_of(blk), in_=vn_of(blk), func=ACT.Abs_reciprocal_sqrt, scale=W_SCALE * W_SCALE)

        def epi_u(blk):
            nc.vector.tensor_tensor(out=r_of(blk), in0=r_of(blk), in1=vn_of(blk), op=ALU.mult)

        def epi_r(blk):
            h, m0, n = blk
            nc.vector.scalar_tensor_tensor(out=r_of(blk), in0=w1t[:, m0 : m0 + n, h * FH : (h + 1) * FH], scalar=-1.0, in1=r_of(blk), op0=ALU.mult, op1=ALU.subtract)

        stat_cols = []

        def epi_sq(blk):
            h, m0, n = blk
            junk = sb.tile([P, 2, FH], BF16, name="junk", bufs=1)
            j = len(stat_cols)
            stat_cols.append(blk)
            nc.scalar.activation(out=junk[:, 0:n, :], in_=r_of(blk), func=ACT.Square, accum_out=stats[:, j : j + 1])


        def w_gram():
            gram = ps_dh.tile([P, P], F32, name="dh")
            for mm in range(NM):
                for b in range(8):
                    blk = w1t[:, mm, b * P : (b + 1) * P]
                    nc.tensor.matmul(out=gram[:], lhsT=blk, rhs=blk, start=(mm == 0 and b == 0), stop=(mm == NM - 1 and b == 7))
            return gram

        with tc.manual_schedule():
            load_a(0, 0)
            nc.sync.dma_start(out=xs[:], in_=xs_v)
            load_x(0, 0)
            load_dy(0)
            load_w(0)
            for q in range(4):
                nc.sync.dma_start(
                    out=ws[32 * q : 32 * q + 4, :, :].bitcast(I32),
                    in_=w2_scales[:, 4 * q : 4 * q + 4, :].rearrange("c r n -> r c n").bitcast(I32),
                )
            load_a(0, 1)
            load_dy(1)
            load_x(1, 0)
            load_a(0, 2)
            load_dy(2)
            load_x(2, 0)
            load_a(0, 3)
            load_dy(3)
            load_x(3, 0)
            load_w(1)
            load_a(1, 0)
            load_x(0, 1)
            load_x(1, 1)
            load_a(1, 1)
            nc.sync.dma_start(out=w1t[:], in_=w1_v)
            load_mv(0, 0)
            load_x(2, 1)
            load_a(1, 2)
            load_x(3, 1)
            load_mv(0, 1)
            load_a(1, 3)
            load_mv(0, 2)
            load_mv(0, 3)
            for k in range(4):
                load_mv(1, k)

            nc.vector.memset(small[:], 0.0)
            nc.scalar.activation(out=small[:, 0:1], in_=small[:, 1:2], func=ACT.Gelu)
            def dy_unit(k):
                return k // 2, k % 2

            clamp(0)
            s_gelu(0)
            x_widen(0, 0)
            for k in range(2 + DY_LEAD):
                dy_transpose(*dy_unit(k))
                dy_copy(*dy_unit(k), 0)
                dy_copy(*dy_unit(k), 1)
                if k == 1:
                    dy_quant(0, 0)
                    x_interleave(0, 0)
                    dy_quant(0, 1)
                    x_quant(0, 0)
            if DY_LEAD:
                dy_transpose(1, 1)
            x_at = {}
            for unit, plan in X_PLAN.items():
                if unit == (0, 0):
                    continue
                step = int(plan[2:])
                x_at.setdefault((step, "w"), []).append(unit)
                if plan[1] == "P":
                    x_at.setdefault((step + 1, "t"), []).append(unit)
                    x_at.setdefault((step + 1 + X_LAG, "c"), []).append(unit)
                    x_at.setdefault((step + 2 + (X_LAG > 0), "q"), []).append(unit)
                else:
                    x_at.setdefault((step + 1, "v"), []).append(unit)
                    x_at.setdefault((step + 2, "q"), []).append(unit)

            for i in range(16):
                h, g, q = i // 8, (i // 2) % 4, i % 2
                if X_FIRST:
                    for unit in x_at.get((i, "t"), []):
                        x_transfer(*unit)
                if i > 0:
                    s_gelu(i)
                g_diff(i)
                for unit in x_at.get((i, "c"), []):
                    x_interleave(*unit)
                for unit in x_at.get((i, "w"), []):
                    x_widen(*unit)
                kq = i + 1 + DY_LEAD
                if 2 <= kq < 8:
                    dy_quant(*dy_unit(kq))
                if q == 0 and i + 2 < 16:
                    clamp(i // 2 + 1)
                if q == 0 and i > 0:
                    v_quant_da(i // 2 - 1)
                for unit in x_at.get((i, "q"), []):
                    x_quant(*unit)
                for unit in x_at.get((i, "v"), []):
                    x_interleave(*unit)
                if i in (11, 13, 15):
                    epi_vn((0, i - 11, 2))
                v_third(i)
                kc = i + 2 + DY_LEAD
                kt = i + 2 + 2 * DY_LEAD
                if DH_FIRST:
                    banks = pe_dh(i)
                if kt < 8:
                    dy_transpose(*dy_unit(kt))
                if h == 1:
                    epi_front(0, i - 8)
                if not DH_FIRST:
                    banks = pe_dh(i)
                if not X_FIRST:
                    for unit in x_at.get((i, "t"), []):
                        x_transfer(*unit)
                if kc < 8:
                    dy_copy(*dy_unit(kc), 0)
                if h == 1:
                    epi_mn(0, i - 8)
                v_da(i, banks)
                if kc < 8:
                    dy_copy(*dy_unit(kc), 1)
            b0 = [(0, 2 * k, 2) for k in range(4)]
            c0 = [(1, 0, 2), (1, 2, 2), (1, 4, 2), (1, 6, 1), (1, 7, 1)]
            for k in range(3):
                epi_rs(b0[k])
            v_quant_da(7)

            def front(mm):
                epi_front(1, mm, *((ps_g, "gps") if mm % 2 == 0 else (ps_dh, "dh")))

            front(0)
            front(1)
            epi_u(b0[0])
            epi_vn(b0[3])
            epi_rs(b0[3])
            epi_u(b0[1])
            epi_r(b0[0])
            epi_sq(b0[0])
            epi_mn(1, 0)
            front(2)
            epi_mn(1, 1)
            front(3)
            epi_u(b0[2])
            epi_r(b0[1])
            epi_vn(c0[0])
            epi_rs(c0[0])
            epi_sq(b0[1])
            epi_mn(1, 2)
            front(4)
            epi_mn(1, 3)
            front(5)
            epi_u(b0[3])
            epi_r(b0[2])
            epi_vn(c0[1])
            epi_rs(c0[1])
            epi_sq(b0[2])
            epi_mn(1, 4)
            front(6)
            epi_u(c0[0])
            epi_mn(1, 5)
            front(7)
            gram = w_gram()
            epi_r(b0[3])
            epi_vn(c0[2])
            epi_rs(c0[2])
            epi_sq(b0[3])
            epi_r(c0[0])
            epi_mn(1, 6)
            epi_mn(1, 7)
            epi_sq(c0[0])
            epi_u(c0[1])
            epi_vn(c0[3])
            epi_rs(c0[3])
            epi_vn(c0[4])
            epi_rs(c0[4])
            epi_r(c0[1])
            epi_sq(c0[1])
            scr = sb.tile([P, P], F32, name="scr", bufs=1)
            nc.vector.tensor_tensor(out=scr[:], in0=gram[:], in1=ident[:], op=ALU.mult)
            epi_u(c0[2])
            nc.vector.tensor_reduce(out=small[:, 2:3], in_=scr[:], op=ALU.add, axis=mybir.AxisListType.X)
            tw = ps_tr.tile([P, 1], F32, name="tr")
            nc.tensor.matmul(out=tw[:], lhsT=ones[:], rhs=small[:, 2:3], start=True, stop=True)
            epi_u(c0[3])
            epi_r(c0[2])
            epi_sq(c0[2])
            nc.vector.tensor_scalar(out=small[:, 3:4], in0=tw[:], scalar1=0.25, scalar2=None, op0=ALU.mult)
            epi_u(c0[4])
            epi_r(c0[3])
            epi_sq(c0[3])
            nc.vector.reciprocal(out=small[:, 4:5], in_=small[:, 3:4])
            epi_r(c0[4])
            epi_sq(c0[4])

            tot = ps_tr.tile([P, 1], F32, name="tr")
            n = len(stat_cols)
            for j in range(n):
                nc.tensor.matmul(out=tot[:], lhsT=ones[:], rhs=stats[:, j : j + 1], start=(j == 0), stop=(j == n - 1))
            nc.scalar.activation(out=small2[:, 0:1], in_=tot[:], func=ACT.Abs_reciprocal_sqrt, scale=small[:, 4:5])
            for mm, f0, f1 in [(0, 0, 256), (0, 256, 1024)] + [(mm, 0, 1024) for mm in range(1, NM)]:
                nc.vector.scalar_tensor_tensor(
                    out=r[:, mm, f0:f1], in0=r[:, mm, f0:f1], scalar=small2[:, 0:1], in1=w1t[:, mm, f0:f1], op0=ALU.mult, op1=ALU.add
                )
                nc.sync.dma_start(out=out_v[:, mm, f0:f1], in_=r[:, mm, f0:f1])
